import numpy as np
import ml_dtypes


def mxq(x, axis, fmt="e4m3"):
    dtype, down = {"e4m3": (ml_dtypes.float8_e4m3fn, 7), "e5m2": (ml_dtypes.float8_e5m2, 14)}[fmt]
    v = np.moveaxis(np.asarray(x, np.float32).astype(ml_dtypes.bfloat16).astype(np.float64), axis, -1)
    blocks = v.reshape(v.shape[:-1] + (-1, 32))
    amax = np.abs(blocks).max(-1, keepdims=True)
    byte = np.maximum(np.where(amax > 0, np.frexp(amax)[1] - 1 + 127, 0) - down, 1)
    scale = np.exp2(byte - 127.0)
    codes = (blocks / scale).astype(np.float32).astype(dtype).astype(np.float64)
    return np.moveaxis((codes * scale).reshape(v.shape), -1, axis)


WIDE = False


def mx_kscale(k):
    if not WIDE:
        return np.ones(k)
    levels = np.array([24, -24, 12, -12, 0])
    if k % 512:
        return np.exp2(np.random.permutation(np.resize(levels, k // 32))).repeat(32)
    a = np.empty((k // 512, 16))
    for p in range(k // 512):
        a[p, :8] = np.random.permutation(np.resize(levels, 8))
        for g in range(8):
            far = levels[np.abs(levels - a[p, g]) >= 10]
            a[p, g + 8] = far[np.random.randint(len(far))]
    return np.exp2(a.ravel()).repeat(32)


def f64(x):
    return np.asarray(x).astype(np.float64)


def striped(idx):
    return np.tile(idx.reshape(-1, 16).T, (8, 1)).astype(np.uint16)


def unstriped(offs):
    return offs[:16].T.reshape(-1).astype(np.int64)


E2M1 = np.array([0.0, 0.5, 1.0, 1.5, 2.0, 3.0, 4.0, 6.0, -0.0, -0.5, -1.0, -1.5, -2.0, -3.0, -4.0, -6.0])


def pack_weight(w, fmt):
    k, n = w.shape
    w = f64(np.asarray(w, np.float32).astype(ml_dtypes.bfloat16)).reshape(k // 32, 32, n)
    amax = np.abs(w).max(1)
    if fmt == "e4m3":
        byte = np.frexp(amax)[1] - 1 + 127 - 7
    else:
        mant, ex = np.frexp(amax / 6.0)
        byte = np.where(mant > 0.5, ex, ex - 1) + 127
    byte = np.clip(np.where(amax > 0, byte, 1), 1, 254)
    scaled = (w * np.exp2(127.0 - byte)[:, None, :]).reshape(k, n).astype(np.float32)
    by_word = np.ascontiguousarray(scaled.reshape(k // 512, 128, 4, n).transpose(0, 1, 3, 2))
    if fmt == "e4m3":
        words = by_word.astype(ml_dtypes.float8_e4m3fn).view(np.uint8)
    else:
        c = by_word.astype(ml_dtypes.float4_e2m1fn).view(np.uint8) & 0xF
        words = (c[..., 0::2] | (c[..., 1::2] << 4)).reshape(k // 512, 128, 2 * n)
    return np.ascontiguousarray(words), np.ascontiguousarray(byte.astype(np.uint8).reshape(k // 512, 16, n))


def unpack_weight(words, scales, fmt):
    g, _, n = scales.shape
    words = np.ascontiguousarray(words).reshape(g, 128, n, -1)
    if fmt == "e4m3":
        vals = words.view(ml_dtypes.float8_e4m3fn).astype(np.float64)
    else:
        nib = np.empty((g, 128, n, 4), np.uint8)
        nib[..., 0::2] = words & 0xF
        nib[..., 1::2] = words >> 4
        vals = E2M1[nib]
    vals = vals * np.repeat(np.exp2(scales.astype(np.float64) - 127.0), 8, axis=1)[..., None]
    return vals.transpose(0, 1, 3, 2).reshape(g * 512, n)


def pack_table4(v):
    words, scales = pack_weight(v, "e2m1")
    g, t = words.shape[0] // 2, v.shape[1]
    return np.ascontiguousarray(words.reshape(g, 2, 128, t, 2).transpose(0, 2, 3, 1, 4).reshape(g, 128, t, 4)), scales


def unpack_table4(words, scales):
    g, _, t, _ = words.shape
    return unpack_weight(words.reshape(g, 128, t, 2, 2).transpose(0, 3, 1, 2, 4).reshape(2 * g, 128, 2 * t), scales, "e2m1")


def sigm(f):
    return 1.0 / (1.0 + np.exp(-np.maximum(f, -700.0)))


K, L, N, T, J = 1024, 512, 512, 2048, 1024


def setup_inputs():
    n = np.random.standard_normal
    s = mx_kscale(K)[:, None]
    s2 = mx_kscale(L)[:, None]
    p_tab = pack_table4(n((K, T)) * s)
    p_tab2 = pack_weight(n((L, T)) * s2, "e4m3")
    p_zv = pack_weight(n((K, N)) / np.sqrt(K) / s, "e4m3")
    p_zt = pack_weight(n((L, N)) / np.sqrt(L) / s2, "e2m1")
    p_wv = pack_weight(n((K, N)) / np.sqrt(K) / s, "e2m1")
    return {
        "tab_words": p_tab[0],
        "tab_scales": p_tab[1],
        "tab2_words": p_tab2[0],
        "tab2_scales": p_tab2[1],
        "zv_words": p_zv[0],
        "zv_scales": p_zv[1],
        "zt_words": p_zt[0],
        "zt_scales": p_zt[1],
        "b": (0.3 * n(N)).astype(np.float32),
        "wv_words": p_wv[0],
        "wv_scales": p_wv[1],
        "wt": (n((L, N)) / np.sqrt(L) / s2).astype(np.float32),
        "gT": (n((N, T))).astype(np.float32),
        "offs": striped(np.random.permutation(T)[:J]),
        "offs2": striped(np.random.permutation(T)[:J]),
    }


def reference(tab_words, tab_scales, tab2_words, tab2_scales, zv_words, zv_scales, zt_words, zt_scales, b, wv_words, wv_scales, wt, gT, offs, offs2):
    idx = unstriped(offs)
    idx2 = unstriped(offs2)
    tab_ = unpack_table4(tab_words, tab_scales)[:, idx]
    tab2_ = unpack_weight(tab2_words, tab2_scales, "e4m3")[:, idx2]
    zv_ = unpack_weight(zv_words, zv_scales, "e4m3")
    zt_ = unpack_weight(zt_words, zt_scales, "e2m1")
    z = zv_.T @ tab_ + zt_.T @ tab2_
    gate = sigm(z + f64(b)[:, None])
    wv_ = unpack_weight(wv_words, wv_scales, "e2m1")
    wt_ = mxq(f64(wt), 0, "e4m3")
    hv = wv_.T @ tab_
    ht = wt_.T @ tab2_
    av = np.maximum(hv, 0.0)
    at = np.maximum(ht, 0.0)
    return (at + gate * (av - at)) * f64(gT)[:, idx]

@@ -1,0 +1,155 @@
+from contextlib import ExitStack
+
+import concourse.mybir as mybir
+from concourse.masks import make_identity
+
+K, L, N, T, J = 1024, 512, 512, 2048, 1024
+FLOPS = 2 * N * J * (2 * K + 2 * L)
+
+F32 = mybir.dt.float32
+BF16 = mybir.dt.bfloat16
+I32 = mybir.dt.int32
+U32 = mybir.dt.uint32
+U16 = mybir.dt.uint16
+U8 = mybir.dt.uint8
+FP8X4 = mybir.dt.float8_e4m3fn_x4
+FP4X4 = mybir.dt.float4_e2m1fn_x4
+ACT = mybir.ActivationFunctionType
+ALU = mybir.AluOpType
+
+P = 128
+HALF = 512
+HCOL = HALF // 16
+
+
+def tile_list_gmu_relu_gate_kernel(
+    tc, tab_words, tab_scales, tab2_words, tab2_scales, zv_words, zv_scales, zt_words, zt_scales,
+    b, wv_words, wv_scales, wt, gT, offs, offs2, out,
+):
+    nc = tc.nc
+    with ExitStack() as ctx:
+        keep = ctx.enter_context(tc.tile_pool(name="keep", bufs=1))
+        work = ctx.enter_context(tc.tile_pool(name="work", bufs=2))
+        psum = ctx.enter_context(tc.psum_pool(name="psum", bufs=1))
+
+        list1 = keep.tile([P, J // 16], U16, name="list1")
+        list2 = keep.tile([P, J // 16], U16, name="list2")
+        v_words = keep.tile([P, T], U32, name="v_words", align_bytes=64)
+        v2_words = keep.tile([P, T], U32, name="v2_words", align_bytes=64)
+        v_scales = keep.tile([P, T], U8, name="v_scales", align_bytes=64)
+        v2_scales = keep.tile([P, T], U8, name="v2_scales", align_bytes=64)
+        zv_w = keep.tile([P, 2, N], U32, name="zv_w", align_bytes=64)
+        zt_w = keep.tile([P, 2 * N], U8, name="zt_w", align_bytes=64)
+        wv_w = keep.tile([P, 2, 2 * N], U8, name="wv_w", align_bytes=64)
+        zv_s = keep.tile([P, 2, N], U8, name="zv_s", align_bytes=64)
+        zt_s = keep.tile([P, N], U8, name="zt_s", align_bytes=64)
+        wv_s = keep.tile([P, 2, N], U8, name="wv_s", align_bytes=64)
+        wt_raw = keep.tile([P, 4, N], F32, name="wt_raw")
+        wt_bf = keep.tile([P, N, 4], BF16, name="wt_bf", align_bytes=64)
+        wt_w = keep.tile([P, N], U32, name="wt_w", align_bytes=64)
+        wt_s = keep.tile([P, N], U8, name="wt_s", align_bytes=64)
+        b_rows = keep.tile([P, P], F32, name="b_rows")
+        ident = keep.tile([P, P], F32, name="ident")
+        b_pos = keep.tile([P, 4], F32, name="b_pos")
+        b_neg = keep.tile([P, 4], F32, name="b_neg")
+        g_tiles = [keep.tile([P, T], F32, name="g%d" % i) for i in range(4)]
+        pick_s01 = keep.tile([P, J], U8, name="pick_s01", align_bytes=64)
+        pick_s1 = keep.tile([P, J], U8, name="pick_s1", align_bytes=64)
+        pick_pair = [keep.tile([P, HALF], U32, name="pick_pair%d" % h, align_bytes=64) for h in range(2)]
+        pick_v = [keep.tile([P, 2, HALF], U16, name="pick_v%d" % h, align_bytes=64) for h in range(2)]
+        pick_v2 = [keep.tile([P, HALF], U32, name="pick_v2%d" % h, align_bytes=64) for h in range(2)]
+        pick_s2 = [keep.tile([P, HALF], U8, name="pick_s2%d" % h, align_bytes=64) for h in range(2)]
+
+        nc.vector.memset(v_scales[:].bitcast(I32), 0)
+        nc.vector.memset(v2_scales[:].bitcast(I32), 0)
+        nc.vector.memset(zv_s[:].bitcast(I32), 0)
+        nc.vector.memset(zt_s[:].bitcast(I32), 0)
+        nc.vector.memset(wv_s[:].bitcast(I32), 0)
+        nc.vector.memset(pick_s1[:].bitcast(I32), 0)
+        nc.vector.memset(b_rows[:], 0.0)
+        make_identity(nc, ident[:])
+
+        nc.sync.dma_start(list1[:], offs)
+        for q in range(4):
+            nc.sync.dma_start(v_scales[32 * q : 32 * q + 8, :].bitcast(I32), tab_scales[:, 4 * q : 4 * q + 4, :].bitcast(I32))
+        nc.sync.dma_start(v_words[:].bitcast(I32), tab_words[0].rearrange("p t c -> p (t c)").bitcast(I32))
+        nc.sync.dma_start(list2[:], offs2)
+        nc.sync.dma_start(v2_words[:].bitcast(I32), tab2_words[0].rearrange("p t c -> p (t c)").bitcast(I32))
+        for r in range(4):
+            nc.sync.dma_start(v2_scales[r:P:32, :].bitcast(I32), tab2_scales[0, r:16:4, :].bitcast(I32))
+        nc.sync.dma_start(wt_raw[:], wt.rearrange("(p j) n -> p j n", j=4))
+        nc.sync.dma_start(zv_w[:].bitcast(I32), zv_words.rearrange("a p n c -> p a (n c)").bitcast(I32))
+        nc.sync.dma_start(zt_w[:].bitcast(I32), zt_words[0].bitcast(I32))
+        nc.sync.dma_start(wv_w[:].bitcast(I32), wv_words.rearrange("a p m -> p a m").bitcast(I32))
+        nc.sync.dma_start(b_rows[0:4, :], b.rearrange("(c p) -> c p", p=P))
+        for r in range(4):
+            nc.sync.dma_start(zv_s[r:P:32, :, :].bitcast(I32), zv_scales[:, r:16:4, :].rearrange("a q n -> q a n").bitcast(I32))
+        for r in range(4):
+            nc.sync.dma_start(zt_s[r:P:32, :].bitcast(I32), zt_scales[0, r:16:4, :].bitcast(I32))
+        for r in range(4):
+            nc.sync.dma_start(wv_s[r:P:32, :, :].bitcast(I32), wv_scales[:, r:16:4, :].rearrange("a q n -> q a n").bitcast(I32))
+        for i in range(4):
+            nc.sync.dma_start(g_tiles[i][:], gT[P * i : P * (i + 1), :])
+
+        nc.vector.tensor_copy(pick_s01[:], v_scales[:].indirect(list1[:]))
+        for r in range(4):
+            nc.scalar.dma_start(pick_s1[r:P:32, :].bitcast(I32), pick_s01[4 + r : P : 32, :].bitcast(I32))
+
+        b_t = psum.tile([P, HALF], F32, name="b_t", tag="z", bufs=2)
+        nc.tensor.transpose(b_t[:, 0:P], b_rows[:], ident[:])
+        nc.scalar.activation(b_pos[:], b_t[:, 0:4], ACT.Copy)
+        nc.scalar.activation(b_neg[:], b_t[:, 0:4], ACT.Copy, scale=-1.0)
+        nc.scalar.copy(wt_bf[:], wt_raw[:].rearrange("p j n -> p n j"))
+
+        for h in range(2):
+            cols = slice(h * HCOL, (h + 1) * HCOL)
+            nc.vector.tensor_copy(pick_pair[h][:], v_words[:].indirect(list1[:, cols]))
+            nc.vector.tensor_copy(pick_v2[h][:], v2_words[:].indirect(list2[:, cols]))
+            nc.vector.tensor_copy(pick_v[h][:], pick_pair[h][:].bitcast(U16).rearrange("p (t d) -> p d t", d=2))
+            nc.vector.tensor_copy(pick_s2[h][:], v2_scales[:].indirect(list2[:, cols]))
+            if h == 0:
+                nc.vector.quantize_mx(wt_w[:].bitcast(FP8X4), wt_s[:], wt_bf[:].rearrange("p n j -> p (n j)"))
+
+        def products(i, h):
+            n_cols = slice(P * i, P * (i + 1))
+            n_bytes = slice(2 * P * i, 2 * P * (i + 1))
+            j_cols = slice(HALF * h, HALF * (h + 1))
+            v_ops = [(pick_v[h][:, a, :].bitcast(FP4X4), (pick_s01, pick_s1)[a][:, j_cols]) for a in range(2)]
+            v2_op = (pick_v2[h][:].bitcast(FP8X4), pick_s2[h][:])
+            z = psum.tile([P, HALF], F32, name="z", tag="z", bufs=2)
+            hv = psum.tile([P, HALF], F32, name="hv", tag="hv", bufs=3)
+            ht = psum.tile([P, HALF], F32, name="ht", tag="ht", bufs=3)
+            nc.tensor.matmul_mx(z[:], zv_w[:, 0, n_cols].bitcast(FP8X4), zv_s[:, 0, n_cols], v_ops[0][0], v_ops[0][1], start=True, stop=False)
+            nc.tensor.matmul_mx(z[:], zt_w[:, n_bytes].bitcast(FP4X4), zt_s[:, n_cols], v2_op[0], v2_op[1], start=False, stop=False)
+            nc.tensor.matmul_mx(z[:], zv_w[:, 1, n_cols].bitcast(FP8X4), zv_s[:, 1, n_cols], v_ops[1][0], v_ops[1][1], start=False, stop=True)
+            for a in range(2):
+                nc.tensor.matmul_mx(hv[:], wv_w[:, a, n_bytes].bitcast(FP4X4), wv_s[:, a, n_cols], v_ops[a][0], v_ops[a][1], start=(a == 0), stop=(a == 1))
+            nc.tensor.matmul_mx(ht[:], wt_w[:, n_cols].bitcast(FP8X4), wt_s[:, n_cols], v2_op[0], v2_op[1], start=True, stop=True)
+            gate = work.tile([P, HALF], F32, name="gate")
+            rest = work.tile([P, HALF], F32, name="rest")
+            nc.scalar.activation(gate[:], z[:], ACT.Sigmoid, bias=b_pos[:, i : i + 1])
+            nc.scalar.activation(rest[:], z[:], ACT.Sigmoid, bias=b_neg[:, i : i + 1], scale=-1.0)
+            part_v = work.tile([P, HALF], F32, name="part_v")
+            part_t = work.tile([P, HALF], F32, name="part_t")
+            nc.vector.scalar_tensor_tensor(part_v[:], hv[:], 0.0, gate[:], ALU.max, ALU.mult)
+            nc.vector.scalar_tensor_tensor(part_t[:], ht[:], 0.0, rest[:], ALU.max, ALU.mult)
+            return part_v, part_t
+
+        def mix(parts):
+            mixed = work.tile([P, HALF], F32, name="mixed")
+            nc.vector.tensor_tensor(mixed[:], parts[0][:], parts[1][:], ALU.add)
+            return mixed
+
+        def finish(i, h, mixed):
+            res = work.tile([P, HALF], F32, name="res", bufs=4)
+            nc.vector.tensor_tensor(res[:], g_tiles[i][:].indirect(list1[:, h * HCOL : (h + 1) * HCOL]), mixed[:], ALU.mult)
+            nc.sync.dma_start(out[P * i : P * (i + 1), HALF * h : HALF * (h + 1)], res[:])
+
+        units = [(0, 0), (1, 0), (0, 1), (1, 1), (2, 0), (2, 1), (3, 0), (3, 1)]
+        pending = None
+        for i, h in units:
+            parts = products(i, h)
+            if pending is not None:
+                finish(*pending)
+            pending = (i, h, mix(parts))
+        finish(*pending)

@@ -36,70 +36,79 @@ def tile_list_gmu_relu_gate_kernel(
         list2 = keep.tile([P, J // 16], U16, name="list2")
         v_words = keep.tile([P, T], U32, name="v_words", align_bytes=64)
         v2_words = keep.tile([P, T], U32, name="v2_words", align_bytes=64)
-        v_scales = keep.tile([P, T], U8, name="v_scales", align_bytes=64)
-        v2_scales = keep.tile([P, T], U8, name="v2_scales", align_bytes=64)
-        zv_w = keep.tile([P, 2, N], U32, name="zv_w", align_bytes=64)
-        zt_w = keep.tile([P, 2 * N], U8, name="zt_w", align_bytes=64)
-        wv_w = keep.tile([P, 2, 2 * N], U8, name="wv_w", align_bytes=64)
-        zv_s = keep.tile([P, 2, N], U8, name="zv_s", align_bytes=64)
-        zt_s = keep.tile([P, N], U8, name="zt_s", align_bytes=64)
-        wv_s = keep.tile([P, 2, N], U8, name="wv_s", align_bytes=64)
-        wt_raw = keep.tile([P, 4, N], F32, name="wt_raw")
-        wt_bf = keep.tile([P, N, 4], BF16, name="wt_bf", align_bytes=64)
+        v_scales = keep.tile([P, T], U8, name="v_scales", tag="slot_a", align_bytes=64)
+        v2_scales = keep.tile([P, T], U8, name="v2_scales", tag="slot_w", align_bytes=64)
+        w_rows = keep.tile([16, 5, N], U8, name="w_rows", align_bytes=64)
+        w_s = keep.tile([P, 5, N], U8, name="w_s", align_bytes=64)
         wt_w = keep.tile([P, N], U32, name="wt_w", align_bytes=64)
         wt_s = keep.tile([P, N], U8, name="wt_s", align_bytes=64)
         b_rows = keep.tile([P, P], F32, name="b_rows")
         ident = keep.tile([P, P], F32, name="ident")
         b_pos = keep.tile([P, 4], F32, name="b_pos")
         b_neg = keep.tile([P, 4], F32, name="b_neg")
-        g_tiles = [keep.tile([P, T], F32, name="g%d" % i) for i in range(4)]
-        pick_s01 = keep.tile([P, J], U8, name="pick_s01", align_bytes=64)
-        pick_s1 = keep.tile([P, J], U8, name="pick_s1", align_bytes=64)
+        pick_s01 = keep.tile([P, J], U8, name="pick_s01", tag="slot_g", align_bytes=64)
+        pick_s = keep.tile([P, 2, J], U8, name="pick_s", align_bytes=64)
         pick_pair = [keep.tile([P, HALF], U32, name="pick_pair%d" % h, align_bytes=64) for h in range(2)]
         pick_v = [keep.tile([P, 2, HALF], U16, name="pick_v%d" % h, align_bytes=64) for h in range(2)]
         pick_v2 = [keep.tile([P, HALF], U32, name="pick_v2%d" % h, align_bytes=64) for h in range(2)]
         pick_s2 = [keep.tile([P, HALF], U8, name="pick_s2%d" % h, align_bytes=64) for h in range(2)]
 
-        nc.vector.memset(v_scales[:].bitcast(I32), 0)
+        zv_w = keep.tile([P, 2, N], U32, name="zv_w", align_bytes=64)
+        zt_w = keep.tile([P, 2 * N], U8, name="zt_w", align_bytes=64)
+        wv_w = keep.tile([P, 2, 2 * N], U8, name="wv_w", align_bytes=64)
+
         nc.vector.memset(v2_scales[:].bitcast(I32), 0)
-        nc.vector.memset(zv_s[:].bitcast(I32), 0)
-        nc.vector.memset(zt_s[:].bitcast(I32), 0)
-        nc.vector.memset(wv_s[:].bitcast(I32), 0)
-        nc.vector.memset(pick_s1[:].bitcast(I32), 0)
-        nc.vector.memset(b_rows[:], 0.0)
+        nc.vector.memset(w_s[:].bitcast(I32), 0)
+        nc.vector.memset(v_scales[0:96, :].bitcast(I32), 0)
+        nc.vector.memset(pick_s[:].bitcast(I32), 0)
+
+        nc.gpsimd.memset(b_rows[:], 0.0)
         make_identity(nc, ident[:])
+        nc.gpsimd.dma_start(b_rows[0:4, :], b.rearrange("(c p) -> c p", p=P))
+        for r in range(4):
+            nc.gpsimd.dma_start(v2_scales[r:P:32, :].bitcast(I32), tab2_scales[0, r:16:4, :].bitcast(I32))
+        warm = keep.tile([P, 8], F32, name="warm")
+        nc.scalar.activation(warm[:, 0:1], ident[:, 0:1], ACT.Sigmoid)
 
         nc.sync.dma_start(list1[:], offs)
-        for q in range(4):
-            nc.sync.dma_start(v_scales[32 * q : 32 * q + 8, :].bitcast(I32), tab_scales[:, 4 * q : 4 * q + 4, :].bitcast(I32))
+        nc.sync.dma_start(v_scales[96:P, :].bitcast(I32), tab_scales.rearrange("a q t -> (a q) t").bitcast(I32))
+        nc.sync.dma_start(w_rows[:, 0:2, :].bitcast(I32), zv_scales.rearrange("a q n -> q a n").bitcast(I32))
+        nc.sync.dma_start(w_rows[:, 2, :].bitcast(I32), zt_scales[0].bitcast(I32))
+        nc.sync.dma_start(w_rows[:, 3:5, :].bitcast(I32), wv_scales.rearrange("a q n -> q a n").bitcast(I32))
         nc.sync.dma_start(v_words[:].bitcast(I32), tab_words[0].rearrange("p t c -> p (t c)").bitcast(I32))
         nc.sync.dma_start(list2[:], offs2)
         nc.sync.dma_start(v2_words[:].bitcast(I32), tab2_words[0].rearrange("p t c -> p (t c)").bitcast(I32))
-        for r in range(4):
-            nc.sync.dma_start(v2_scales[r:P:32, :].bitcast(I32), tab2_scales[0, r:16:4, :].bitcast(I32))
-        nc.sync.dma_start(wt_raw[:], wt.rearrange("(p j) n -> p j n", j=4))
         nc.sync.dma_start(zv_w[:].bitcast(I32), zv_words.rearrange("a p n c -> p a (n c)").bitcast(I32))
         nc.sync.dma_start(zt_w[:].bitcast(I32), zt_words[0].bitcast(I32))
         nc.sync.dma_start(wv_w[:].bitcast(I32), wv_words.rearrange("a p m -> p a m").bitcast(I32))
-        nc.sync.dma_start(b_rows[0:4, :], b.rearrange("(c p) -> c p", p=P))
         for r in range(4):
-            nc.sync.dma_start(zv_s[r:P:32, :, :].bitcast(I32), zv_scales[:, r:16:4, :].rearrange("a q n -> q a n").bitcast(I32))
-        for r in range(4):
-            nc.sync.dma_start(zt_s[r:P:32, :].bitcast(I32), zt_scales[0, r:16:4, :].bitcast(I32))
-        for r in range(4):
-            nc.sync.dma_start(wv_s[r:P:32, :, :].bitcast(I32), wv_scales[:, r:16:4, :].rearrange("a q n -> q a n").bitcast(I32))
-        for i in range(4):
-            nc.sync.dma_start(g_tiles[i][:], gT[P * i : P * (i + 1), :])
+            nc.sync.dma_start(w_s[r:P:32, :, :].bitcast(I32), w_rows[r:16:4, :, :].bitcast(I32))
 
         nc.vector.tensor_copy(pick_s01[:], v_scales[:].indirect(list1[:]))
-        for r in range(4):
-            nc.scalar.dma_start(pick_s1[r:P:32, :].bitcast(I32), pick_s01[4 + r : P : 32, :].bitcast(I32))
+        for a in range(2):
+            for r in range(4):
+                first = 96 + 16 * a + r
+                nc.sync.dma_start(pick_s[r:P:32, a, :].bitcast(I32), pick_s01[first : first + 13 : 4, :].bitcast(I32))
+        wt_raw = keep.tile([P, 4, N], F32, name="wt_raw", tag="slot_a", align_bytes=64)
+        nc.sync.dma_start(wt_raw[:], wt.rearrange("(p j) n -> p j n", j=4))
 
-        b_t = psum.tile([P, HALF], F32, name="b_t", tag="z", bufs=2)
+        b_t = psum.tile([P, HALF], F32, name="b_t", tag="ht", bufs=3)
         nc.tensor.transpose(b_t[:, 0:P], b_rows[:], ident[:])
         nc.scalar.activation(b_pos[:], b_t[:, 0:4], ACT.Copy)
         nc.scalar.activation(b_neg[:], b_t[:, 0:4], ACT.Copy, scale=-1.0)
-        nc.scalar.copy(wt_bf[:], wt_raw[:].rearrange("p j n -> p n j"))
+
+        def quantise_wt(cut, copy):
+            wt_bf = keep.tile([P, cut.stop - cut.start, 4], BF16, name="wt_bf%d" % cut.start, align_bytes=64)
+            copy(wt_bf[:], wt_raw[:, :, cut].rearrange("p j n -> p n j"))
+            nc.vector.quantize_mx(wt_w[:, cut].bitcast(FP8X4), wt_s[:, cut], wt_bf[:].rearrange("p n j -> p (n j)"))
+
+        g_tiles = {}
+
+        def load_g(i, slot):
+            g_tiles[i] = keep.tile([P, T], F32, name="g%d" % i, tag=slot, align_bytes=64)
+            nc.sync.dma_start(g_tiles[i][:], gT[P * i : P * (i + 1), :])
+
+        load_g(0, "slot_g")
 
         for h in range(2):
             cols = slice(h * HCOL, (h + 1) * HCOL)
@@ -107,23 +116,23 @@ def tile_list_gmu_relu_gate_kernel(
             nc.vector.tensor_copy(pick_v2[h][:], v2_words[:].indirect(list2[:, cols]))
             nc.vector.tensor_copy(pick_v[h][:], pick_pair[h][:].bitcast(U16).rearrange("p (t d) -> p d t", d=2))
             nc.vector.tensor_copy(pick_s2[h][:], v2_scales[:].indirect(list2[:, cols]))
-            if h == 0:
-                nc.vector.quantize_mx(wt_w[:].bitcast(FP8X4), wt_s[:], wt_bf[:].rearrange("p n j -> p (n j)"))
+
+        load_g(1, "slot_w")
 
         def products(i, h):
             n_cols = slice(P * i, P * (i + 1))
             n_bytes = slice(2 * P * i, 2 * P * (i + 1))
             j_cols = slice(HALF * h, HALF * (h + 1))
-            v_ops = [(pick_v[h][:, a, :].bitcast(FP4X4), (pick_s01, pick_s1)[a][:, j_cols]) for a in range(2)]
+            v_ops = [(pick_v[h][:, a, :].bitcast(FP4X4), pick_s[:, a, j_cols]) for a in range(2)]
             v2_op = (pick_v2[h][:].bitcast(FP8X4), pick_s2[h][:])
             z = psum.tile([P, HALF], F32, name="z", tag="z", bufs=2)
             hv = psum.tile([P, HALF], F32, name="hv", tag="hv", bufs=3)
             ht = psum.tile([P, HALF], F32, name="ht", tag="ht", bufs=3)
-            nc.tensor.matmul_mx(z[:], zv_w[:, 0, n_cols].bitcast(FP8X4), zv_s[:, 0, n_cols], v_ops[0][0], v_ops[0][1], start=True, stop=False)
-            nc.tensor.matmul_mx(z[:], zt_w[:, n_bytes].bitcast(FP4X4), zt_s[:, n_cols], v2_op[0], v2_op[1], start=False, stop=False)
-            nc.tensor.matmul_mx(z[:], zv_w[:, 1, n_cols].bitcast(FP8X4), zv_s[:, 1, n_cols], v_ops[1][0], v_ops[1][1], start=False, stop=True)
+            nc.tensor.matmul_mx(z[:], zv_w[:, 0, n_cols].bitcast(FP8X4), w_s[:, 0, n_cols], v_ops[0][0], v_ops[0][1], start=True, stop=False)
+            nc.tensor.matmul_mx(z[:], zv_w[:, 1, n_cols].bitcast(FP8X4), w_s[:, 1, n_cols], v_ops[1][0], v_ops[1][1], start=False, stop=False)
+            nc.tensor.matmul_mx(z[:], zt_w[:, n_bytes].bitcast(FP4X4), w_s[:, 2, n_cols], v2_op[0], v2_op[1], start=False, stop=True)
             for a in range(2):
-                nc.tensor.matmul_mx(hv[:], wv_w[:, a, n_bytes].bitcast(FP4X4), wv_s[:, a, n_cols], v_ops[a][0], v_ops[a][1], start=(a == 0), stop=(a == 1))
+                nc.tensor.matmul_mx(hv[:], wv_w[:, a, n_bytes].bitcast(FP4X4), w_s[:, 3 + a, n_cols], v_ops[a][0], v_ops[a][1], start=(a == 0), stop=(a == 1))
             nc.tensor.matmul_mx(ht[:], wt_w[:, n_cols].bitcast(FP8X4), wt_s[:, n_cols], v2_op[0], v2_op[1], start=True, stop=True)
             gate = work.tile([P, HALF], F32, name="gate")
             rest = work.tile([P, HALF], F32, name="rest")
@@ -148,8 +157,17 @@ def tile_list_gmu_relu_gate_kernel(
         units = [(0, 0), (1, 0), (0, 1), (1, 1), (2, 0), (2, 1), (3, 0), (3, 1)]
         pending = None
         for i, h in units:
+            if (i, h) == (0, 0):
+                quantise_wt(slice(0, P), nc.vector.tensor_copy)
+            if (i, h) == (1, 0):
+                quantise_wt(slice(P, 2 * P), nc.scalar.copy)
+            if (i, h) == (0, 1):
+                quantise_wt(slice(2 * P, N), nc.scalar.copy)
+                load_g(2, "slot_a")
             parts = products(i, h)
             if pending is not None:
                 finish(*pending)
+                if pending[0:2] == (0, 1):
+                    load_g(3, "slot_g")
             pending = (i, h, mix(parts))
         finish(*pending)

@@ -18,8 +18,15 @@ ACT = mybir.ActivationFunctionType
 ALU = mybir.AluOpType
 
 P = 128
+PACK = 4
 HALF = 512
-HCOL = HALF // 16
+HALF_COLS = HALF // 16
+BLOCKS = 16
+QUAD = 32
+V_ROWS = P - 2 * BLOCKS
+ZV_PLANE, ZT_PLANE, WV_PLANE, W_PLANES = 0, 2, 3, 5
+RING = 4
+GPSIMD_UNITS = 6
 
 
 def tile_list_gmu_relu_gate_kernel(
@@ -36,45 +43,42 @@ def tile_list_gmu_relu_gate_kernel(
         list2 = keep.tile([P, J // 16], U16, name="list2")
         v_words = keep.tile([P, T], U32, name="v_words", align_bytes=64)
         v2_words = keep.tile([P, T], U32, name="v2_words", align_bytes=64)
-        v_scales = keep.tile([P, T], U8, name="v_scales", tag="slot_a", align_bytes=64)
-        v2_scales = keep.tile([P, T], U8, name="v2_scales", tag="slot_w", align_bytes=64)
-        w_rows = keep.tile([16, 5, N], U8, name="w_rows", align_bytes=64)
-        w_s = keep.tile([P, 5, N], U8, name="w_s", align_bytes=64)
-        wt_w = keep.tile([P, N], U32, name="wt_w", align_bytes=64)
-        wt_s = keep.tile([P, N], U8, name="wt_s", align_bytes=64)
+        v_scale_rows = keep.tile([P, T], U8, name="v_scale_rows", tag="wt_slot", align_bytes=64)
+        v2_plane = keep.tile([P, T], U8, name="v2_plane", tag="g1_slot", align_bytes=64)
+        w_rows = keep.tile([BLOCKS, W_PLANES, N], U8, name="w_rows", align_bytes=64)
+        w_planes = keep.tile([P, W_PLANES, N], U8, name="w_planes", align_bytes=64)
+        wt_words = keep.tile([P, N], U32, name="wt_words", align_bytes=64)
+        wt_plane = keep.tile([P, N], U8, name="wt_plane", align_bytes=64)
         b_rows = keep.tile([P, P], F32, name="b_rows")
         ident = keep.tile([P, P], F32, name="ident")
-        b_pos = keep.tile([P, 4], F32, name="b_pos")
-        b_neg = keep.tile([P, 4], F32, name="b_neg")
-        pick_s01 = keep.tile([P, J], U8, name="pick_s01", tag="slot_g", align_bytes=64)
-        pick_s = keep.tile([P, 2, J], U8, name="pick_s", align_bytes=64)
-        pick_pair = [keep.tile([P, HALF], U32, name="pick_pair%d" % h, align_bytes=64) for h in range(2)]
-        pick_v = [keep.tile([P, 2, HALF], U16, name="pick_v%d" % h, align_bytes=64) for h in range(2)]
-        pick_v2 = [keep.tile([P, HALF], U32, name="pick_v2%d" % h, align_bytes=64) for h in range(2)]
-        pick_s2 = [keep.tile([P, HALF], U8, name="pick_s2%d" % h, align_bytes=64) for h in range(2)]
-
+        b_pos = keep.tile([P, N // P], F32, name="b_pos")
+        b_neg = keep.tile([P, N // P], F32, name="b_neg")
+        picked_rows = keep.tile([P, J], U8, name="picked_rows", tag="g0_slot", align_bytes=64)
+        picked_planes = keep.tile([P, 2, J], U8, name="picked_planes", align_bytes=64)
+        picked_pairs = [keep.tile([P, HALF], U32, name="picked_pairs%d" % h, align_bytes=64) for h in range(2)]
+        picked_v = [keep.tile([P, 2, HALF], U16, name="picked_v%d" % h, align_bytes=64) for h in range(2)]
+        picked_v2 = [keep.tile([P, HALF], U32, name="picked_v2%d" % h, align_bytes=64) for h in range(2)]
+        picked_plane2 = [keep.tile([P, HALF], U8, name="picked_plane2%d" % h, align_bytes=64) for h in range(2)]
         zv_w = keep.tile([P, 2, N], U32, name="zv_w", align_bytes=64)
         zt_w = keep.tile([P, 2 * N], U8, name="zt_w", align_bytes=64)
         wv_w = keep.tile([P, 2, 2 * N], U8, name="wv_w", align_bytes=64)
 
-        nc.vector.memset(v2_scales[:].bitcast(I32), 0)
-        nc.vector.memset(w_s[:].bitcast(I32), 0)
-        nc.vector.memset(v_scales[0:96, :].bitcast(I32), 0)
-        nc.vector.memset(pick_s[:].bitcast(I32), 0)
+        nc.vector.memset(v2_plane[:].bitcast(I32), 0)
+        nc.vector.memset(w_planes[:].bitcast(I32), 0)
+        nc.vector.memset(v_scale_rows[0:V_ROWS, :].bitcast(I32), 0)
+        nc.vector.memset(picked_planes[:].bitcast(I32), 0)
 
         nc.gpsimd.memset(b_rows[:], 0.0)
         make_identity(nc, ident[:])
-        nc.gpsimd.dma_start(b_rows[0:4, :], b.rearrange("(c p) -> c p", p=P))
+        nc.gpsimd.dma_start(b_rows[0 : N // P, :], b.rearrange("(c p) -> c p", p=P))
         for r in range(4):
-            nc.gpsimd.dma_start(v2_scales[r:P:32, :].bitcast(I32), tab2_scales[0, r:16:4, :].bitcast(I32))
-        warm = keep.tile([P, 8], F32, name="warm")
-        nc.scalar.activation(warm[:, 0:1], ident[:, 0:1], ACT.Sigmoid)
+            nc.gpsimd.dma_start(v2_plane[r:P:QUAD, :].bitcast(I32), tab2_scales[0, r:BLOCKS:4, :].bitcast(I32))
 
         nc.sync.dma_start(list1[:], offs)
-        nc.sync.dma_start(v_scales[96:P, :].bitcast(I32), tab_scales.rearrange("a q t -> (a q) t").bitcast(I32))
-        nc.sync.dma_start(w_rows[:, 0:2, :].bitcast(I32), zv_scales.rearrange("a q n -> q a n").bitcast(I32))
-        nc.sync.dma_start(w_rows[:, 2, :].bitcast(I32), zt_scales[0].bitcast(I32))
-        nc.sync.dma_start(w_rows[:, 3:5, :].bitcast(I32), wv_scales.rearrange("a q n -> q a n").bitcast(I32))
+        nc.sync.dma_start(v_scale_rows[V_ROWS:P, :].bitcast(I32), tab_scales.rearrange("a q t -> (a q) t").bitcast(I32))
+        nc.sync.dma_start(w_rows[:, ZV_PLANE:ZT_PLANE, :].bitcast(I32), zv_scales.rearrange("a q n -> q a n").bitcast(I32))
+        nc.sync.dma_start(w_rows[:, ZT_PLANE, :].bitcast(I32), zt_scales[0].bitcast(I32))
+        nc.sync.dma_start(w_rows[:, WV_PLANE:W_PLANES, :].bitcast(I32), wv_scales.rearrange("a q n -> q a n").bitcast(I32))
         nc.sync.dma_start(v_words[:].bitcast(I32), tab_words[0].rearrange("p t c -> p (t c)").bitcast(I32))
         nc.sync.dma_start(list2[:], offs2)
         nc.sync.dma_start(v2_words[:].bitcast(I32), tab2_words[0].rearrange("p t c -> p (t c)").bitcast(I32))
@@ -82,25 +86,30 @@ def tile_list_gmu_relu_gate_kernel(
         nc.sync.dma_start(zt_w[:].bitcast(I32), zt_words[0].bitcast(I32))
         nc.sync.dma_start(wv_w[:].bitcast(I32), wv_words.rearrange("a p m -> p a m").bitcast(I32))
         for r in range(4):
-            nc.sync.dma_start(w_s[r:P:32, :, :].bitcast(I32), w_rows[r:16:4, :, :].bitcast(I32))
+            nc.sync.dma_start(w_planes[r:P:QUAD, :, :].bitcast(I32), w_rows[r:BLOCKS:4, :, :].bitcast(I32))
 
-        nc.vector.tensor_copy(pick_s01[:], v_scales[:].indirect(list1[:]))
+        nc.vector.tensor_copy(picked_rows[:], v_scale_rows[:].indirect(list1[:]))
+        wt_raw = keep.tile([P, PACK, N], F32, name="wt_raw", tag="wt_slot", align_bytes=64)
         for a in range(2):
             for r in range(4):
-                first = 96 + 16 * a + r
-                nc.sync.dma_start(pick_s[r:P:32, a, :].bitcast(I32), pick_s01[first : first + 13 : 4, :].bitcast(I32))
-        wt_raw = keep.tile([P, 4, N], F32, name="wt_raw", tag="slot_a", align_bytes=64)
-        nc.sync.dma_start(wt_raw[:], wt.rearrange("(p j) n -> p j n", j=4))
+                first = V_ROWS + BLOCKS * a + r
+                nc.sync.dma_start(
+                    picked_planes[r:P:QUAD, a, :].bitcast(I32),
+                    picked_rows[first : V_ROWS + BLOCKS * (a + 1) : 4, :].bitcast(I32),
+                )
+        nc.sync.dma_start(wt_raw[:], wt.rearrange("(p j) n -> p j n", j=PACK))
 
-        b_t = psum.tile([P, HALF], F32, name="b_t", tag="ht", bufs=3)
-        nc.tensor.transpose(b_t[:, 0:P], b_rows[:], ident[:])
-        nc.scalar.activation(b_pos[:], b_t[:, 0:4], ACT.Copy)
-        nc.scalar.activation(b_neg[:], b_t[:, 0:4], ACT.Copy, scale=-1.0)
+        b_turned = psum.tile([P, HALF], F32, name="b_turned", tag="ht", bufs=3)
+        nc.tensor.transpose(b_turned[:, 0:P], b_rows[:], ident[:])
+        nc.vector.tensor_copy(b_pos[:], b_turned[:, 0 : N // P])
+        nc.vector.tensor_scalar_mul(b_neg[:], b_turned[:, 0 : N // P], -1.0)
 
-        def quantise_wt(cut, copy):
-            wt_bf = keep.tile([P, cut.stop - cut.start, 4], BF16, name="wt_bf%d" % cut.start, align_bytes=64)
+        def quantise_wt(cut, copy, slot):
+            wt_bf = keep.tile([P, cut.stop - cut.start, PACK], BF16, name="wt_bf", tag=slot, align_bytes=64)
             copy(wt_bf[:], wt_raw[:, :, cut].rearrange("p j n -> p n j"))
-            nc.vector.quantize_mx(wt_w[:, cut].bitcast(FP8X4), wt_s[:, cut], wt_bf[:].rearrange("p n j -> p (n j)"))
+            nc.vector.quantize_mx(
+                wt_words[:, cut].bitcast(FP8X4), wt_plane[:, cut], wt_bf[:].rearrange("p n j -> p (n j)")
+            )
 
         g_tiles = {}
 
@@ -108,66 +117,91 @@ def tile_list_gmu_relu_gate_kernel(
             g_tiles[i] = keep.tile([P, T], F32, name="g%d" % i, tag=slot, align_bytes=64)
             nc.sync.dma_start(g_tiles[i][:], gT[P * i : P * (i + 1), :])
 
-        load_g(0, "slot_g")
+        load_g(0, "g0_slot")
 
         for h in range(2):
-            cols = slice(h * HCOL, (h + 1) * HCOL)
-            nc.vector.tensor_copy(pick_pair[h][:], v_words[:].indirect(list1[:, cols]))
-            nc.vector.tensor_copy(pick_v2[h][:], v2_words[:].indirect(list2[:, cols]))
-            nc.vector.tensor_copy(pick_v[h][:], pick_pair[h][:].bitcast(U16).rearrange("p (t d) -> p d t", d=2))
-            nc.vector.tensor_copy(pick_s2[h][:], v2_scales[:].indirect(list2[:, cols]))
+            cols = slice(h * HALF_COLS, (h + 1) * HALF_COLS)
+            nc.vector.tensor_copy(picked_pairs[h][:], v_words[:].indirect(list1[:, cols]))
+            nc.vector.tensor_copy(picked_v2[h][:], v2_words[:].indirect(list2[:, cols]))
+            nc.vector.tensor_copy(picked_v[h][:], picked_pairs[h][:].bitcast(U16).rearrange("p (t d) -> p d t", d=2))
+            nc.vector.tensor_copy(picked_plane2[h][:], v2_plane[:].indirect(list2[:, cols]))
 
-        load_g(1, "slot_w")
+        load_g(1, "g1_slot")
 
-        def products(i, h):
+        def products(unit, i, h):
             n_cols = slice(P * i, P * (i + 1))
             n_bytes = slice(2 * P * i, 2 * P * (i + 1))
             j_cols = slice(HALF * h, HALF * (h + 1))
-            v_ops = [(pick_v[h][:, a, :].bitcast(FP4X4), pick_s[:, a, j_cols]) for a in range(2)]
-            v2_op = (pick_v2[h][:].bitcast(FP8X4), pick_s2[h][:])
+            v_codes = [picked_v[h][:, a, :].bitcast(FP4X4) for a in range(2)]
+            v_planes = [picked_planes[:, a, j_cols] for a in range(2)]
+            v2_codes = picked_v2[h][:].bitcast(FP8X4)
             z = psum.tile([P, HALF], F32, name="z", tag="z", bufs=2)
             hv = psum.tile([P, HALF], F32, name="hv", tag="hv", bufs=3)
             ht = psum.tile([P, HALF], F32, name="ht", tag="ht", bufs=3)
-            nc.tensor.matmul_mx(z[:], zv_w[:, 0, n_cols].bitcast(FP8X4), w_s[:, 0, n_cols], v_ops[0][0], v_ops[0][1], start=True, stop=False)
-            nc.tensor.matmul_mx(z[:], zv_w[:, 1, n_cols].bitcast(FP8X4), w_s[:, 1, n_cols], v_ops[1][0], v_ops[1][1], start=False, stop=False)
-            nc.tensor.matmul_mx(z[:], zt_w[:, n_bytes].bitcast(FP4X4), w_s[:, 2, n_cols], v2_op[0], v2_op[1], start=False, stop=True)
             for a in range(2):
-                nc.tensor.matmul_mx(hv[:], wv_w[:, a, n_bytes].bitcast(FP4X4), w_s[:, 3 + a, n_cols], v_ops[a][0], v_ops[a][1], start=(a == 0), stop=(a == 1))
-            nc.tensor.matmul_mx(ht[:], wt_w[:, n_cols].bitcast(FP8X4), wt_s[:, n_cols], v2_op[0], v2_op[1], start=True, stop=True)
-            gate = work.tile([P, HALF], F32, name="gate")
-            rest = work.tile([P, HALF], F32, name="rest")
+                nc.tensor.matmul_mx(
+                    z[:], zv_w[:, a, n_cols].bitcast(FP8X4), w_planes[:, ZV_PLANE + a, n_cols],
+                    v_codes[a], v_planes[a], start=(a == 0), stop=False,
+                )
+            nc.tensor.matmul_mx(
+                z[:], zt_w[:, n_bytes].bitcast(FP4X4), w_planes[:, ZT_PLANE, n_cols],
+                v2_codes, picked_plane2[h][:], start=False, stop=True,
+            )
+            for a in range(2):
+                nc.tensor.matmul_mx(
+                    hv[:], wv_w[:, a, n_bytes].bitcast(FP4X4), w_planes[:, WV_PLANE + a, n_cols],
+                    v_codes[a], v_planes[a], start=(a == 0), stop=(a == 1),
+                )
+            nc.tensor.matmul_mx(
+                ht[:], wt_words[:, n_cols].bitcast(FP8X4), wt_plane[:, n_cols],
+                v2_codes, picked_plane2[h][:], start=True, stop=True,
+            )
+            gate = keep.tile([P, HALF], F32, name="gate", tag="gate%d" % (unit % RING))
+            rest = keep.tile([P, HALF], F32, name="rest", tag="rest%d" % (unit % RING), align_bytes=64)
             nc.scalar.activation(gate[:], z[:], ACT.Sigmoid, bias=b_pos[:, i : i + 1])
             nc.scalar.activation(rest[:], z[:], ACT.Sigmoid, bias=b_neg[:, i : i + 1], scale=-1.0)
-            part_v = work.tile([P, HALF], F32, name="part_v")
-            part_t = work.tile([P, HALF], F32, name="part_t")
+            part_v = work.tile([P, HALF], F32, name="part_v", bufs=RING)
+            part_t = work.tile([P, HALF], F32, name="part_t", bufs=RING)
             nc.vector.scalar_tensor_tensor(part_v[:], hv[:], 0.0, gate[:], ALU.max, ALU.mult)
             nc.vector.scalar_tensor_tensor(part_t[:], ht[:], 0.0, rest[:], ALU.max, ALU.mult)
             return part_v, part_t
 
-        def mix(parts):
-            mixed = work.tile([P, HALF], F32, name="mixed")
-            nc.vector.tensor_tensor(mixed[:], parts[0][:], parts[1][:], ALU.add)
-            return mixed
-
-        def finish(i, h, mixed):
-            res = work.tile([P, HALF], F32, name="res", bufs=4)
-            nc.vector.tensor_tensor(res[:], g_tiles[i][:].indirect(list1[:, h * HCOL : (h + 1) * HCOL]), mixed[:], ALU.mult)
+        def store(i, h, res):
             nc.sync.dma_start(out[P * i : P * (i + 1), HALF * h : HALF * (h + 1)], res[:])
 
-        units = [(0, 0), (1, 0), (0, 1), (1, 1), (2, 0), (2, 1), (3, 0), (3, 1)]
-        pending = None
-        for i, h in units:
-            if (i, h) == (0, 0):
-                quantise_wt(slice(0, P), nc.vector.tensor_copy)
-            if (i, h) == (1, 0):
-                quantise_wt(slice(P, 2 * P), nc.scalar.copy)
-            if (i, h) == (0, 1):
-                quantise_wt(slice(2 * P, N), nc.scalar.copy)
-                load_g(2, "slot_a")
-            parts = products(i, h)
-            if pending is not None:
-                finish(*pending)
-                if pending[0:2] == (0, 1):
-                    load_g(3, "slot_g")
-            pending = (i, h, mix(parts))
-        finish(*pending)
+        def listed_g(i, h):
+            return g_tiles[i][:].indirect(list1[:, h * HALF_COLS : (h + 1) * HALF_COLS])
+
+        units = [(i, h) for i in range(N // P) for h in range(2)]
+        left = []
+        for unit, (i, h) in enumerate(units):
+            if unit == 0:
+                quantise_wt(slice(0, P), nc.vector.tensor_copy, "wt_bf")
+            part_v, part_t = products(unit, i, h)
+            if unit == 0:
+                quantise_wt(slice(P, 2 * P), nc.scalar.copy, "rest0")
+            if unit == 1:
+                quantise_wt(slice(2 * P, N), nc.scalar.copy, "rest1")
+                load_g(2, "wt_slot")
+            if unit < GPSIMD_UNITS:
+                factor = keep.tile([P, HALF], F32, name="factor", tag="gate%d" % (unit % RING))
+                nc.vector.tensor_copy(factor[:], listed_g(i, h))
+                if unit == 1:
+                    load_g(3, "g0_slot")
+                mixed = work.tile([P, HALF], F32, name="mixed")
+                nc.gpsimd.tensor_tensor(mixed[:], part_v[:], part_t[:], ALU.add)
+                res = work.tile([P, HALF], F32, name="res", bufs=RING)
+                nc.gpsimd.tensor_tensor(res[:], mixed[:], factor[:], ALU.mult)
+                store(i, h, res)
+            else:
+                left.append((i, h, part_v, part_t))
+
+        totals = []
+        for i, h, part_v, part_t in left:
+            total = work.tile([P, HALF], F32, name="total")
+            nc.vector.tensor_tensor(total[:], part_v[:], part_t[:], ALU.add)
+            totals.append(total)
+        for (i, h, part_v, part_t), total in zip(left, totals):
+            res = work.tile([P, HALF], F32, name="res", bufs=RING)
+            nc.vector.tensor_tensor(res[:], listed_g(i, h), total[:], ALU.mult)
+            store(i, h, res)

@@ -26,7 +26,7 @@ QUAD = 32
 V_ROWS = P - 2 * BLOCKS
 ZV_PLANE, ZT_PLANE, WV_PLANE, W_PLANES = 0, 2, 3, 5
 RING = 4
-GPSIMD_UNITS = 6
+GPSIMD_UNITS = 7
 
 
 def tile_list_gmu_relu_gate_kernel(
@@ -172,6 +172,11 @@ def tile_list_gmu_relu_gate_kernel(
         def listed_g(i, h):
             return g_tiles[i][:].indirect(list1[:, h * HALF_COLS : (h + 1) * HALF_COLS])
 
+        def finish(i, h, total):
+            res = work.tile([P, HALF], F32, name="res", bufs=RING)
+            nc.vector.tensor_tensor(res[:], listed_g(i, h), total[:], ALU.mult)
+            store(i, h, res)
+
         units = [(i, h) for i in range(N // P) for h in range(2)]
         left = []
         for unit, (i, h) in enumerate(units):
@@ -183,25 +188,12 @@ def tile_list_gmu_relu_gate_kernel(
             if unit == 1:
                 quantise_wt(slice(2 * P, N), nc.scalar.copy, "rest1")
                 load_g(2, "wt_slot")
-            if unit < GPSIMD_UNITS:
-                factor = keep.tile([P, HALF], F32, name="factor", tag="gate%d" % (unit % RING))
-                nc.vector.tensor_copy(factor[:], listed_g(i, h))
-                if unit == 1:
-                    load_g(3, "g0_slot")
-                mixed = work.tile([P, HALF], F32, name="mixed")
-                nc.gpsimd.tensor_tensor(mixed[:], part_v[:], part_t[:], ALU.add)
-                res = work.tile([P, HALF], F32, name="res", bufs=RING)
-                nc.gpsimd.tensor_tensor(res[:], mixed[:], factor[:], ALU.mult)
-                store(i, h, res)
-            else:
-                left.append((i, h, part_v, part_t))
-
-        totals = []
-        for i, h, part_v, part_t in left:
-            total = work.tile([P, HALF], F32, name="total")
-            nc.vector.tensor_tensor(total[:], part_v[:], part_t[:], ALU.add)
-            totals.append(total)
-        for (i, h, part_v, part_t), total in zip(left, totals):
-            res = work.tile([P, HALF], F32, name="res", bufs=RING)
-            nc.vector.tensor_tensor(res[:], listed_g(i, h), total[:], ALU.mult)
-            store(i, h, res)
+            total = work.tile([P, HALF], F32, name="total", bufs=RING)
+            add = nc.gpsimd.tensor_tensor if unit < GPSIMD_UNITS else nc.vector.tensor_tensor
+            add(total[:], part_v[:], part_t[:], ALU.add)
+            if left:
+                finish(*left.pop())
+            left.append((i, h, total))
+            if unit == 2:
+                load_g(3, "g0_slot")
+        finish(*left.pop())

@@ -25,8 +25,9 @@ BLOCKS = 16
 QUAD = 32
 V_ROWS = P - 2 * BLOCKS
 ZV_PLANE, ZT_PLANE, WV_PLANE, W_PLANES = 0, 2, 3, 5
-RING = 4
+RING = 8
 GPSIMD_UNITS = 7
+LAG = 2
 
 
 def tile_list_gmu_relu_gate_kernel(
@@ -41,75 +42,59 @@ def tile_list_gmu_relu_gate_kernel(
 
         list1 = keep.tile([P, J // 16], U16, name="list1")
         list2 = keep.tile([P, J // 16], U16, name="list2")
-        v_words = keep.tile([P, T], U32, name="v_words", align_bytes=64)
-        v2_words = keep.tile([P, T], U32, name="v2_words", align_bytes=64)
-        v_scale_rows = keep.tile([P, T], U8, name="v_scale_rows", tag="wt_slot", align_bytes=64)
-        v2_plane = keep.tile([P, T], U8, name="v2_plane", tag="g1_slot", align_bytes=64)
-        w_rows = keep.tile([BLOCKS, W_PLANES, N], U8, name="w_rows", align_bytes=64)
+        v_scale_rows = keep.tile([P, T], U8, name="v_scale_rows", tag="slot_a", align_bytes=64)
+        v2_scale_rows = keep.tile([P, T], U8, name="v2_scale_rows", tag="slot_b", align_bytes=64)
+        w_rows = keep.tile([BLOCKS, W_PLANES, N], U8, name="w_rows", tag="slot_c", align_bytes=64)
+        wt_raw = keep.tile([P, PACK, N], F32, name="wt_raw", tag="slot_d", align_bytes=64)
+        v2_words = keep.tile([P, T], U32, name="v2_words", tag="slot_e", align_bytes=64)
+        picked_rows = keep.tile([P, 2, J], U8, name="picked_rows", tag="slot_f", align_bytes=64)
         w_planes = keep.tile([P, W_PLANES, N], U8, name="w_planes", align_bytes=64)
-        wt_words = keep.tile([P, N], U32, name="wt_words", align_bytes=64)
         wt_plane = keep.tile([P, N], U8, name="wt_plane", align_bytes=64)
         b_rows = keep.tile([P, P], F32, name="b_rows")
         ident = keep.tile([P, P], F32, name="ident")
         b_pos = keep.tile([P, N // P], F32, name="b_pos")
         b_neg = keep.tile([P, N // P], F32, name="b_neg")
-        picked_rows = keep.tile([P, J], U8, name="picked_rows", tag="g0_slot", align_bytes=64)
-        picked_planes = keep.tile([P, 2, J], U8, name="picked_planes", align_bytes=64)
-        picked_pairs = [keep.tile([P, HALF], U32, name="picked_pairs%d" % h, align_bytes=64) for h in range(2)]
+        picked_planes = keep.tile([P, 2, 2 * J], U8, name="picked_planes", align_bytes=64)
         picked_v = [keep.tile([P, 2, HALF], U16, name="picked_v%d" % h, align_bytes=64) for h in range(2)]
-        picked_v2 = [keep.tile([P, HALF], U32, name="picked_v2%d" % h, align_bytes=64) for h in range(2)]
-        picked_plane2 = [keep.tile([P, HALF], U8, name="picked_plane2%d" % h, align_bytes=64) for h in range(2)]
         zv_w = keep.tile([P, 2, N], U32, name="zv_w", align_bytes=64)
         zt_w = keep.tile([P, 2 * N], U8, name="zt_w", align_bytes=64)
-        wv_w = keep.tile([P, 2, 2 * N], U8, name="wv_w", align_bytes=64)
 
-        nc.vector.memset(v2_plane[:].bitcast(I32), 0)
-        nc.vector.memset(w_planes[:].bitcast(I32), 0)
         nc.vector.memset(v_scale_rows[0:V_ROWS, :].bitcast(I32), 0)
+        nc.vector.memset(w_planes[:].bitcast(I32), 0)
         nc.vector.memset(picked_planes[:].bitcast(I32), 0)
 
+        nc.gpsimd.memset(v2_scale_rows[:].bitcast(I32), 0)
+        nc.scalar.dma_start(v2_scale_rows[V_ROWS:P:2, :].bitcast(I32), tab2_scales[0].bitcast(I32))
         nc.gpsimd.memset(b_rows[:], 0.0)
-        make_identity(nc, ident[:])
         nc.gpsimd.dma_start(b_rows[0 : N // P, :], b.rearrange("(c p) -> c p", p=P))
-        for r in range(4):
-            nc.gpsimd.dma_start(v2_plane[r:P:QUAD, :].bitcast(I32), tab2_scales[0, r:BLOCKS:4, :].bitcast(I32))
+        make_identity(nc, ident[:])
 
         nc.sync.dma_start(list1[:], offs)
-        nc.sync.dma_start(v_scale_rows[V_ROWS:P, :].bitcast(I32), tab_scales.rearrange("a q t -> (a q) t").bitcast(I32))
+        nc.sync.dma_start(v_scale_rows[V_ROWS:P, :].bitcast(I32), tab_scales.rearrange("a q t -> q a t").bitcast(I32))
+        nc.sync.dma_start(list2[:], offs2)
         nc.sync.dma_start(w_rows[:, ZV_PLANE:ZT_PLANE, :].bitcast(I32), zv_scales.rearrange("a q n -> q a n").bitcast(I32))
         nc.sync.dma_start(w_rows[:, ZT_PLANE, :].bitcast(I32), zt_scales[0].bitcast(I32))
         nc.sync.dma_start(w_rows[:, WV_PLANE:W_PLANES, :].bitcast(I32), wv_scales.rearrange("a q n -> q a n").bitcast(I32))
-        nc.sync.dma_start(v_words[:].bitcast(I32), tab_words[0].rearrange("p t c -> p (t c)").bitcast(I32))
-        nc.sync.dma_start(list2[:], offs2)
-        nc.sync.dma_start(v2_words[:].bitcast(I32), tab2_words[0].rearrange("p t c -> p (t c)").bitcast(I32))
-        nc.sync.dma_start(zv_w[:].bitcast(I32), zv_words.rearrange("a p n c -> p a (n c)").bitcast(I32))
-        nc.sync.dma_start(zt_w[:].bitcast(I32), zt_words[0].bitcast(I32))
-        nc.sync.dma_start(wv_w[:].bitcast(I32), wv_words.rearrange("a p m -> p a m").bitcast(I32))
-        for r in range(4):
-            nc.sync.dma_start(w_planes[r:P:QUAD, :, :].bitcast(I32), w_rows[r:BLOCKS:4, :, :].bitcast(I32))
-
-        nc.vector.tensor_copy(picked_rows[:], v_scale_rows[:].indirect(list1[:]))
-        wt_raw = keep.tile([P, PACK, N], F32, name="wt_raw", tag="wt_slot", align_bytes=64)
-        for a in range(2):
-            for r in range(4):
-                first = V_ROWS + BLOCKS * a + r
-                nc.sync.dma_start(
-                    picked_planes[r:P:QUAD, a, :].bitcast(I32),
-                    picked_rows[first : V_ROWS + BLOCKS * (a + 1) : 4, :].bitcast(I32),
-                )
         nc.sync.dma_start(wt_raw[:], wt.rearrange("(p j) n -> p j n", j=PACK))
+        nc.sync.dma_start(v2_words[:].bitcast(I32), tab2_words[0].rearrange("p t c -> p (t c)").bitcast(I32))
+        nc.sync.dma_start(zt_w[:].bitcast(I32), zt_words[0].bitcast(I32))
+        nc.sync.dma_start(zv_w[:].bitcast(I32), zv_words.rearrange("a p n c -> p a (n c)").bitcast(I32))
 
-        b_turned = psum.tile([P, HALF], F32, name="b_turned", tag="ht", bufs=3)
-        nc.tensor.transpose(b_turned[:, 0:P], b_rows[:], ident[:])
-        nc.vector.tensor_copy(b_pos[:], b_turned[:, 0 : N // P])
-        nc.vector.tensor_scalar_mul(b_neg[:], b_turned[:, 0 : N // P], -1.0)
+        for r in range(4):
+            nc.scalar.dma_start(w_planes[r:P:QUAD, :, :].bitcast(I32), w_rows[r:BLOCKS:4, :, :].bitcast(I32))
 
-        def quantise_wt(cut, copy, slot):
-            wt_bf = keep.tile([P, cut.stop - cut.start, PACK], BF16, name="wt_bf", tag=slot, align_bytes=64)
-            copy(wt_bf[:], wt_raw[:, :, cut].rearrange("p j n -> p n j"))
-            nc.vector.quantize_mx(
-                wt_words[:, cut].bitcast(FP8X4), wt_plane[:, cut], wt_bf[:].rearrange("p n j -> p (n j)")
+        nc.vector.tensor_copy(picked_rows[:, 0, :], v_scale_rows[:].indirect(list1[:]))
+        v_words = keep.tile([P, T], U32, name="v_words", tag="slot_a", align_bytes=64)
+        nc.sync.dma_start(v_words[:].bitcast(I32), tab_words[0].rearrange("p t c -> p (t c)").bitcast(I32))
+        nc.vector.tensor_copy(picked_rows[:, 1, :], v2_scale_rows[:].indirect(list2[:]))
+        for quad in range(4):
+            first = V_ROWS + 8 * quad
+            nc.sync.dma_start(
+                picked_planes[QUAD * quad : QUAD * quad + 4, :, :].bitcast(I32),
+                picked_rows[first : first + 8, :, :].rearrange("p s j -> p (s j)").bitcast(I32),
             )
+        wv_w = keep.tile([P, 2, 2 * N], U8, name="wv_w", tag="slot_c", align_bytes=64)
+        nc.sync.dma_start(wv_w[:].bitcast(I32), wv_words.rearrange("a p m -> p a m").bitcast(I32))
 
         g_tiles = {}
 
@@ -117,16 +102,31 @@ def tile_list_gmu_relu_gate_kernel(
             g_tiles[i] = keep.tile([P, T], F32, name="g%d" % i, tag=slot, align_bytes=64)
             nc.sync.dma_start(g_tiles[i][:], gT[P * i : P * (i + 1), :])
 
-        load_g(0, "g0_slot")
+        picked_v2 = keep.tile([P, J], U32, name="picked_v2", tag="slot_b", align_bytes=64)
+        nc.vector.tensor_copy(picked_v2[:], v2_words[:].indirect(list2[:]))
+        wt_words = keep.tile([P, N], U32, name="wt_words", tag="slot_e", align_bytes=64)
+
+        for h in range(2):
+            cut = slice(h * N // 2, (h + 1) * N // 2)
+            wt_bf = keep.tile([P, N // 2, PACK], BF16, name="wt_bf%d" % h, align_bytes=64)
+            nc.scalar.copy(wt_bf[:], wt_raw[:, :, cut].rearrange("p j n -> p n j"))
+            nc.vector.quantize_mx(
+                wt_words[:, cut].bitcast(FP8X4), wt_plane[:, cut], wt_bf[:].rearrange("p n j -> p (n j)")
+            )
 
         for h in range(2):
             cols = slice(h * HALF_COLS, (h + 1) * HALF_COLS)
-            nc.vector.tensor_copy(picked_pairs[h][:], v_words[:].indirect(list1[:, cols]))
-            nc.vector.tensor_copy(picked_v2[h][:], v2_words[:].indirect(list2[:, cols]))
-            nc.vector.tensor_copy(picked_v[h][:], picked_pairs[h][:].bitcast(U16).rearrange("p (t d) -> p d t", d=2))
-            nc.vector.tensor_copy(picked_plane2[h][:], v2_plane[:].indirect(list2[:, cols]))
+            picked_pairs = keep.tile([P, HALF], U32, name="picked_pairs", align_bytes=64)
+            nc.vector.tensor_copy(picked_pairs[:], v_words[:].indirect(list1[:, cols]))
+            nc.vector.tensor_copy(picked_v[h][:], picked_pairs[:].bitcast(U16).rearrange("p (t d) -> p d t", d=2))
 
-        load_g(1, "g1_slot")
+        for i, slot in enumerate(("slot_f", "slot_d", "wt_bf0", "slot_a")):
+            load_g(i, slot)
+
+        b_turned = psum.tile([P, HALF], F32, name="b_turned", tag="hv", bufs=3)
+        nc.tensor.transpose(b_turned[:, 0:P], b_rows[:], ident[:])
+        nc.scalar.copy(b_pos[:], b_turned[:, 0 : N // P])
+        nc.scalar.activation(b_neg[:], b_turned[:, 0 : N // P], ACT.Copy, scale=-1.0)
 
         def products(unit, i, h):
             n_cols = slice(P * i, P * (i + 1))
@@ -134,19 +134,20 @@ def tile_list_gmu_relu_gate_kernel(
             j_cols = slice(HALF * h, HALF * (h + 1))
             v_codes = [picked_v[h][:, a, :].bitcast(FP4X4) for a in range(2)]
             v_planes = [picked_planes[:, a, j_cols] for a in range(2)]
-            v2_codes = picked_v2[h][:].bitcast(FP8X4)
+            v2_codes = picked_v2[:, j_cols].bitcast(FP8X4)
+            v2_plane = picked_planes[:, 0, J + HALF * h : J + HALF * (h + 1)]
             z = psum.tile([P, HALF], F32, name="z", tag="z", bufs=2)
             hv = psum.tile([P, HALF], F32, name="hv", tag="hv", bufs=3)
             ht = psum.tile([P, HALF], F32, name="ht", tag="ht", bufs=3)
+            nc.tensor.matmul_mx(
+                z[:], zt_w[:, n_bytes].bitcast(FP4X4), w_planes[:, ZT_PLANE, n_cols],
+                v2_codes, v2_plane, start=True, stop=False,
+            )
             for a in range(2):
                 nc.tensor.matmul_mx(
                     z[:], zv_w[:, a, n_cols].bitcast(FP8X4), w_planes[:, ZV_PLANE + a, n_cols],
-                    v_codes[a], v_planes[a], start=(a == 0), stop=False,
+                    v_codes[a], v_planes[a], start=False, stop=(a == 1),
                 )
-            nc.tensor.matmul_mx(
-                z[:], zt_w[:, n_bytes].bitcast(FP4X4), w_planes[:, ZT_PLANE, n_cols],
-                v2_codes, picked_plane2[h][:], start=False, stop=True,
-            )
             for a in range(2):
                 nc.tensor.matmul_mx(
                     hv[:], wv_w[:, a, n_bytes].bitcast(FP4X4), w_planes[:, WV_PLANE + a, n_cols],
@@ -154,13 +155,13 @@ def tile_list_gmu_relu_gate_kernel(
                 )
             nc.tensor.matmul_mx(
                 ht[:], wt_words[:, n_cols].bitcast(FP8X4), wt_plane[:, n_cols],
-                v2_codes, picked_plane2[h][:], start=True, stop=True,
+                v2_codes, v2_plane, start=True, stop=True,
             )
             gate = keep.tile([P, HALF], F32, name="gate", tag="gate%d" % (unit % RING))
             rest = keep.tile([P, HALF], F32, name="rest", tag="rest%d" % (unit % RING), align_bytes=64)
             nc.scalar.activation(gate[:], z[:], ACT.Sigmoid, bias=b_pos[:, i : i + 1])
             nc.scalar.activation(rest[:], z[:], ACT.Sigmoid, bias=b_neg[:, i : i + 1], scale=-1.0)
-            part_v = work.tile([P, HALF], F32, name="part_v", bufs=RING)
+            part_v = work.tile([P, HALF], F32, name="part_v", bufs=LAG + 1)
             part_t = work.tile([P, HALF], F32, name="part_t", bufs=RING)
             nc.vector.scalar_tensor_tensor(part_v[:], hv[:], 0.0, gate[:], ALU.max, ALU.mult)
             nc.vector.scalar_tensor_tensor(part_t[:], ht[:], 0.0, rest[:], ALU.max, ALU.mult)
@@ -172,28 +173,24 @@ def tile_list_gmu_relu_gate_kernel(
         def listed_g(i, h):
             return g_tiles[i][:].indirect(list1[:, h * HALF_COLS : (h + 1) * HALF_COLS])
 
-        def finish(i, h, total):
-            res = work.tile([P, HALF], F32, name="res", bufs=RING)
-            nc.vector.tensor_tensor(res[:], listed_g(i, h), total[:], ALU.mult)
+        units = [(i, h) for h in range(2) for i in range(N // P)]
+        totals = []
+
+        def finish(unit):
+            i, h = units[unit]
+            if unit + LAG < len(units):
+                res = keep.tile([P, HALF], F32, name="res", tag="rest%d" % ((unit + LAG) % RING), align_bytes=64)
+            else:
+                res = work.tile([P, HALF], F32, name="res")
+            nc.vector.tensor_tensor(res[:], listed_g(i, h), totals[unit][:], ALU.mult)
             store(i, h, res)
 
-        units = [(i, h) for i in range(N // P) for h in range(2)]
-        left = []
         for unit, (i, h) in enumerate(units):
-            if unit == 0:
-                quantise_wt(slice(0, P), nc.vector.tensor_copy, "wt_bf")
             part_v, part_t = products(unit, i, h)
-            if unit == 0:
-                quantise_wt(slice(P, 2 * P), nc.scalar.copy, "rest0")
-            if unit == 1:
-                quantise_wt(slice(2 * P, N), nc.scalar.copy, "rest1")
-                load_g(2, "wt_slot")
-            total = work.tile([P, HALF], F32, name="total", bufs=RING)
+            if unit >= LAG:
+                finish(unit - LAG)
             add = nc.gpsimd.tensor_tensor if unit < GPSIMD_UNITS else nc.vector.tensor_tensor
-            add(total[:], part_v[:], part_t[:], ALU.add)
-            if left:
-                finish(*left.pop())
-            left.append((i, h, total))
-            if unit == 2:
-                load_g(3, "g0_slot")
-        finish(*left.pop())
+            add(part_v[:], part_v[:], part_t[:], ALU.add)
+            totals.append(part_v)
+        for unit in range(len(units) - LAG, len(units)):
+            finish(unit)

@@ -26,8 +26,8 @@ QUAD = 32
 V_ROWS = P - 2 * BLOCKS
 ZV_PLANE, ZT_PLANE, WV_PLANE, W_PLANES = 0, 2, 3, 5
 RING = 8
-GPSIMD_UNITS = 7
-LAG = 2
+GPSIMD_UNITS = 5
+GPSIMD_FINISHED = 2
 
 
 def tile_list_gmu_relu_gate_kernel(
@@ -45,7 +45,7 @@ def tile_list_gmu_relu_gate_kernel(
         v_scale_rows = keep.tile([P, T], U8, name="v_scale_rows", tag="slot_a", align_bytes=64)
         v2_scale_rows = keep.tile([P, T], U8, name="v2_scale_rows", tag="slot_b", align_bytes=64)
         w_rows = keep.tile([BLOCKS, W_PLANES, N], U8, name="w_rows", tag="slot_c", align_bytes=64)
-        wt_raw = keep.tile([P, PACK, N], F32, name="wt_raw", tag="slot_d", align_bytes=64)
+        wv_w = keep.tile([P, 2, 2 * N], U8, name="wv_w", align_bytes=64)
         v2_words = keep.tile([P, T], U32, name="v2_words", tag="slot_e", align_bytes=64)
         picked_rows = keep.tile([P, 2, J], U8, name="picked_rows", tag="slot_f", align_bytes=64)
         w_planes = keep.tile([P, W_PLANES, N], U8, name="w_planes", align_bytes=64)
@@ -56,15 +56,18 @@ def tile_list_gmu_relu_gate_kernel(
         b_neg = keep.tile([P, N // P], F32, name="b_neg")
         picked_planes = keep.tile([P, 2, 2 * J], U8, name="picked_planes", align_bytes=64)
         picked_v = [keep.tile([P, 2, HALF], U16, name="picked_v%d" % h, align_bytes=64) for h in range(2)]
-        zv_w = keep.tile([P, 2, N], U32, name="zv_w", align_bytes=64)
+        v_words = keep.tile([P, T], U32, name="v_words", tag="slot_g", align_bytes=64)
         zt_w = keep.tile([P, 2 * N], U8, name="zt_w", align_bytes=64)
 
+        warm = keep.tile([P, 2], F32, name="warm")
+        nc.vector.memset(warm[:, 0:1], 0.0)
         nc.vector.memset(v_scale_rows[0:V_ROWS, :].bitcast(I32), 0)
         nc.vector.memset(w_planes[:].bitcast(I32), 0)
         nc.vector.memset(picked_planes[:].bitcast(I32), 0)
 
         nc.gpsimd.memset(v2_scale_rows[:].bitcast(I32), 0)
         nc.scalar.dma_start(v2_scale_rows[V_ROWS:P:2, :].bitcast(I32), tab2_scales[0].bitcast(I32))
+        nc.scalar.activation(warm[:, 1:2], warm[:, 0:1], ACT.Sigmoid)
         nc.gpsimd.memset(b_rows[:], 0.0)
         nc.gpsimd.dma_start(b_rows[0 : N // P, :], b.rearrange("(c p) -> c p", p=P))
         make_identity(nc, ident[:])
@@ -75,17 +78,17 @@ def tile_list_gmu_relu_gate_kernel(
         nc.sync.dma_start(w_rows[:, ZV_PLANE:ZT_PLANE, :].bitcast(I32), zv_scales.rearrange("a q n -> q a n").bitcast(I32))
         nc.sync.dma_start(w_rows[:, ZT_PLANE, :].bitcast(I32), zt_scales[0].bitcast(I32))
         nc.sync.dma_start(w_rows[:, WV_PLANE:W_PLANES, :].bitcast(I32), wv_scales.rearrange("a q n -> q a n").bitcast(I32))
-        nc.sync.dma_start(wt_raw[:], wt.rearrange("(p j) n -> p j n", j=PACK))
         nc.sync.dma_start(v2_words[:].bitcast(I32), tab2_words[0].rearrange("p t c -> p (t c)").bitcast(I32))
+        nc.sync.dma_start(v_words[:].bitcast(I32), tab_words[0].rearrange("p t c -> p (t c)").bitcast(I32))
         nc.sync.dma_start(zt_w[:].bitcast(I32), zt_words[0].bitcast(I32))
-        nc.sync.dma_start(zv_w[:].bitcast(I32), zv_words.rearrange("a p n c -> p a (n c)").bitcast(I32))
+        nc.sync.dma_start(wv_w[:].bitcast(I32), wv_words.rearrange("a p m -> p a m").bitcast(I32))
 
         for r in range(4):
             nc.scalar.dma_start(w_planes[r:P:QUAD, :, :].bitcast(I32), w_rows[r:BLOCKS:4, :, :].bitcast(I32))
 
         nc.vector.tensor_copy(picked_rows[:, 0, :], v_scale_rows[:].indirect(list1[:]))
-        v_words = keep.tile([P, T], U32, name="v_words", tag="slot_a", align_bytes=64)
-        nc.sync.dma_start(v_words[:].bitcast(I32), tab_words[0].rearrange("p t c -> p (t c)").bitcast(I32))
+        zv_w = keep.tile([P, 2, N], U32, name="zv_w", tag="slot_a", align_bytes=64)
+        nc.sync.dma_start(zv_w[:].bitcast(I32), zv_words.rearrange("a p n c -> p a (n c)").bitcast(I32))
         nc.vector.tensor_copy(picked_rows[:, 1, :], v2_scale_rows[:].indirect(list2[:]))
         for quad in range(4):
             first = V_ROWS + 8 * quad
@@ -93,8 +96,8 @@ def tile_list_gmu_relu_gate_kernel(
                 picked_planes[QUAD * quad : QUAD * quad + 4, :, :].bitcast(I32),
                 picked_rows[first : first + 8, :, :].rearrange("p s j -> p (s j)").bitcast(I32),
             )
-        wv_w = keep.tile([P, 2, 2 * N], U8, name="wv_w", tag="slot_c", align_bytes=64)
-        nc.sync.dma_start(wv_w[:].bitcast(I32), wv_words.rearrange("a p m -> p a m").bitcast(I32))
+        wt_raw = keep.tile([P, PACK, N], F32, name="wt_raw", tag="slot_c", align_bytes=64)
+        nc.sync.dma_start(wt_raw[:], wt.rearrange("(p j) n -> p j n", j=PACK))
 
         g_tiles = {}
 
@@ -102,10 +105,20 @@ def tile_list_gmu_relu_gate_kernel(
             g_tiles[i] = keep.tile([P, T], F32, name="g%d" % i, tag=slot, align_bytes=64)
             nc.sync.dma_start(g_tiles[i][:], gT[P * i : P * (i + 1), :])
 
-        picked_v2 = keep.tile([P, J], U32, name="picked_v2", tag="slot_b", align_bytes=64)
-        nc.vector.tensor_copy(picked_v2[:], v2_words[:].indirect(list2[:]))
-        wt_words = keep.tile([P, N], U32, name="wt_words", tag="slot_e", align_bytes=64)
+        def gather_words(h, v2_out, pairs):
+            cols = slice(h * HALF_COLS, (h + 1) * HALF_COLS)
+            nc.vector.tensor_copy(v2_out, v2_words[:].indirect(list2[:, cols]))
+            nc.vector.tensor_copy(pairs, v_words[:].indirect(list1[:, cols]))
+            nc.vector.tensor_copy(picked_v[h][:], pairs.bitcast(U16).rearrange("p (t d) -> p d t", d=2))
 
+        first_v2 = keep.tile([P, HALF], U32, name="first_v2", tag="slot_b", align_bytes=64)
+        first_pairs = keep.tile([P, HALF], U32, name="first_pairs", tag="slot_d", align_bytes=64)
+        gather_words(0, first_v2[:], first_pairs[:])
+        second_words = keep.tile([P, 2, HALF], U32, name="second_words", tag="slot_d", align_bytes=64)
+        gather_words(1, second_words[:, 0, :], second_words[:, 1, :])
+        picked_v2 = [first_v2[:], second_words[:, 0, :]]
+
+        wt_words = keep.tile([P, N], U32, name="wt_words", align_bytes=64)
         for h in range(2):
             cut = slice(h * N // 2, (h + 1) * N // 2)
             wt_bf = keep.tile([P, N // 2, PACK], BF16, name="wt_bf%d" % h, align_bytes=64)
@@ -114,13 +127,7 @@ def tile_list_gmu_relu_gate_kernel(
                 wt_words[:, cut].bitcast(FP8X4), wt_plane[:, cut], wt_bf[:].rearrange("p n j -> p (n j)")
             )
 
-        for h in range(2):
-            cols = slice(h * HALF_COLS, (h + 1) * HALF_COLS)
-            picked_pairs = keep.tile([P, HALF], U32, name="picked_pairs", align_bytes=64)
-            nc.vector.tensor_copy(picked_pairs[:], v_words[:].indirect(list1[:, cols]))
-            nc.vector.tensor_copy(picked_v[h][:], picked_pairs[:].bitcast(U16).rearrange("p (t d) -> p d t", d=2))
-
-        for i, slot in enumerate(("slot_f", "slot_d", "wt_bf0", "slot_a")):
+        for i, slot in enumerate(("slot_f", "slot_e", "slot_g", "slot_c")):
             load_g(i, slot)
 
         b_turned = psum.tile([P, HALF], F32, name="b_turned", tag="hv", bufs=3)
@@ -134,7 +141,7 @@ def tile_list_gmu_relu_gate_kernel(
             j_cols = slice(HALF * h, HALF * (h + 1))
             v_codes = [picked_v[h][:, a, :].bitcast(FP4X4) for a in range(2)]
             v_planes = [picked_planes[:, a, j_cols] for a in range(2)]
-            v2_codes = picked_v2[:, j_cols].bitcast(FP8X4)
+            v2_codes = picked_v2[h].bitcast(FP8X4)
             v2_plane = picked_planes[:, 0, J + HALF * h : J + HALF * (h + 1)]
             z = psum.tile([P, HALF], F32, name="z", tag="z", bufs=2)
             hv = psum.tile([P, HALF], F32, name="hv", tag="hv", bufs=3)
@@ -161,36 +168,44 @@ def tile_list_gmu_relu_gate_kernel(
             rest = keep.tile([P, HALF], F32, name="rest", tag="rest%d" % (unit % RING), align_bytes=64)
             nc.scalar.activation(gate[:], z[:], ACT.Sigmoid, bias=b_pos[:, i : i + 1])
             nc.scalar.activation(rest[:], z[:], ACT.Sigmoid, bias=b_neg[:, i : i + 1], scale=-1.0)
-            part_v = work.tile([P, HALF], F32, name="part_v", bufs=LAG + 1)
-            part_t = work.tile([P, HALF], F32, name="part_t", bufs=RING)
-            nc.vector.scalar_tensor_tensor(part_v[:], hv[:], 0.0, gate[:], ALU.max, ALU.mult)
-            nc.vector.scalar_tensor_tensor(part_t[:], ht[:], 0.0, rest[:], ALU.max, ALU.mult)
-            return part_v, part_t
-
-        def store(i, h, res):
-            nc.sync.dma_start(out[P * i : P * (i + 1), HALF * h : HALF * (h + 1)], res[:])
-
-        def listed_g(i, h):
-            return g_tiles[i][:].indirect(list1[:, h * HALF_COLS : (h + 1) * HALF_COLS])
+            nc.vector.scalar_tensor_tensor(part_v[:, unit, :], hv[:], 0.0, gate[:], ALU.max, ALU.mult)
+            nc.vector.scalar_tensor_tensor(part_t[:, unit, :], ht[:], 0.0, rest[:], ALU.max, ALU.mult)
 
         units = [(i, h) for h in range(2) for i in range(N // P)]
-        totals = []
+        part_v = keep.tile([P, len(units), HALF], F32, name="part_v")
+        part_t = keep.tile([P, len(units), HALF], F32, name="part_t")
 
-        def finish(unit):
+        def listed_g(i, h, cut=slice(0, HALF)):
+            return g_tiles[i][:].indirect(list1[:, (h * HALF + cut.start) // 16 : (h * HALF + cut.stop) // 16])
+
+        def store(i, h, res, cut=slice(0, HALF)):
+            nc.sync.dma_start(out[P * i : P * (i + 1), HALF * h + cut.start : HALF * h + cut.stop], res)
+
+        def finish_on_gpsimd(unit):
             i, h = units[unit]
-            if unit + LAG < len(units):
-                res = keep.tile([P, HALF], F32, name="res", tag="rest%d" % ((unit + LAG) % RING), align_bytes=64)
-            else:
-                res = work.tile([P, HALF], F32, name="res")
-            nc.vector.tensor_tensor(res[:], listed_g(i, h), totals[unit][:], ALU.mult)
-            store(i, h, res)
+            factor = keep.tile([P, HALF], F32, name="factor", tag="rest%d" % (unit + 1), align_bytes=64)
+            nc.vector.tensor_copy(factor[:], listed_g(i, h))
+            early = work.tile([P, HALF], F32, name="early")
+            nc.gpsimd.tensor_tensor(early[:], part_v[:, unit, :], factor[:], ALU.mult)
+            store(i, h, early[:])
 
         for unit, (i, h) in enumerate(units):
-            part_v, part_t = products(unit, i, h)
-            if unit >= LAG:
-                finish(unit - LAG)
-            add = nc.gpsimd.tensor_tensor if unit < GPSIMD_UNITS else nc.vector.tensor_tensor
-            add(part_v[:], part_v[:], part_t[:], ALU.add)
-            totals.append(part_v)
-        for unit in range(len(units) - LAG, len(units)):
-            finish(unit)
+            products(unit, i, h)
+            if 0 < unit <= GPSIMD_FINISHED:
+                finish_on_gpsimd(unit - 1)
+            if unit < GPSIMD_UNITS:
+                nc.gpsimd.tensor_tensor(part_v[:, unit, :], part_v[:, unit, :], part_t[:, unit, :], ALU.add)
+
+        res = keep.tile([P, len(units), HALF], F32, name="res", tag="rest%d" % (len(units) - 1), align_bytes=64)
+        for unit in range(GPSIMD_FINISHED, len(units)):
+            i, h = units[unit]
+            pieces = 2 if unit == len(units) - 1 else 1
+            for piece in range(pieces):
+                cut = slice(piece * HALF // pieces, (piece + 1) * HALF // pieces)
+                nc.vector.tensor_tensor(res[:, unit, cut], listed_g(i, h, cut), part_v[:, unit, cut], ALU.mult)
+                store(i, h, res[:, unit, cut], cut)
+            if unit == GPSIMD_FINISHED:
+                rest_units = slice(GPSIMD_UNITS, len(units))
+                nc.vector.tensor_tensor(
+                    part_v[:, rest_units, :], part_v[:, rest_units, :], part_t[:, rest_units, :], ALU.add
+                )

@@ -26,7 +26,7 @@ QUAD = 32
 V_ROWS = P - 2 * BLOCKS
 ZV_PLANE, ZT_PLANE, WV_PLANE, W_PLANES = 0, 2, 3, 5
 RING = 8
-GPSIMD_UNITS = 5
+GPSIMD_UNITS = 4
 GPSIMD_FINISHED = 2
 
 
@@ -196,16 +196,30 @@ def tile_list_gmu_relu_gate_kernel(
             if unit < GPSIMD_UNITS:
                 nc.gpsimd.tensor_tensor(part_v[:, unit, :], part_v[:, unit, :], part_t[:, unit, :], ALU.add)
 
+        totals = [part_v[:, unit, :] for unit in range(GPSIMD_UNITS)]
+        for unit in range(GPSIMD_UNITS, len(units)):
+            turned = psum.tile([P, HALF], F32, name="turned", tag="hv", bufs=3)
+            for c in range(HALF // P):
+                block = slice(P * c, P * (c + 1))
+                for part, first in ((part_v, True), (part_t, False)):
+                    nc.tensor.matmul(
+                        turned[:, block], part[:, unit, block], ident[:], start=first, stop=not first, is_transpose=True
+                    )
+            turned_sum = work.tile([P, HALF], F32, name="turned_sum")
+            nc.scalar.copy(turned_sum[:], turned[:])
+            back = psum.tile([P, HALF], F32, name="back", tag="z", bufs=2)
+            for c in range(HALF // P):
+                block = slice(P * c, P * (c + 1))
+                nc.tensor.transpose(back[:, block], turned_sum[:, block], ident[:])
+            total = work.tile([P, HALF], F32, name="total", bufs=len(units) - GPSIMD_UNITS)
+            nc.scalar.copy(total[:], back[:])
+            totals.append(total[:])
+
         res = keep.tile([P, len(units), HALF], F32, name="res", tag="rest%d" % (len(units) - 1), align_bytes=64)
         for unit in range(GPSIMD_FINISHED, len(units)):
             i, h = units[unit]
             pieces = 2 if unit == len(units) - 1 else 1
             for piece in range(pieces):
                 cut = slice(piece * HALF // pieces, (piece + 1) * HALF // pieces)
-                nc.vector.tensor_tensor(res[:, unit, cut], listed_g(i, h, cut), part_v[:, unit, cut], ALU.mult)
+                nc.vector.tensor_tensor(res[:, unit, cut], listed_g(i, h, cut), totals[unit][:, cut], ALU.mult)
                 store(i, h, res[:, unit, cut], cut)
-            if unit == GPSIMD_FINISHED:
-                rest_units = slice(GPSIMD_UNITS, len(units))
-                nc.vector.tensor_tensor(
-                    part_v[:, rest_units, :], part_v[:, rest_units, :], part_t[:, rest_units, :], ALU.add
-                )

@@ -20,14 +20,15 @@ ALU = mybir.AluOpType
 P = 128
 PACK = 4
 HALF = 512
-HALF_COLS = HALF // 16
+STRIPE = 16
 BLOCKS = 16
 QUAD = 32
-V_ROWS = P - 2 * BLOCKS
+LIVE = 4
+SCALE_ROWS = P - 2 * BLOCKS
 ZV_PLANE, ZT_PLANE, WV_PLANE, W_PLANES = 0, 2, 3, 5
-RING = 8
-GPSIMD_UNITS = 4
-GPSIMD_FINISHED = 2
+Z_BANKS, H_BANKS = 2, 3
+GPSIMD_ADDS = 5
+GPSIMD_FINISHES = 2
 
 
 def tile_list_gmu_relu_gate_kernel(
@@ -40,14 +41,14 @@ def tile_list_gmu_relu_gate_kernel(
         work = ctx.enter_context(tc.tile_pool(name="work", bufs=2))
         psum = ctx.enter_context(tc.psum_pool(name="psum", bufs=1))
 
-        list1 = keep.tile([P, J // 16], U16, name="list1")
-        list2 = keep.tile([P, J // 16], U16, name="list2")
-        v_scale_rows = keep.tile([P, T], U8, name="v_scale_rows", tag="slot_a", align_bytes=64)
-        v2_scale_rows = keep.tile([P, T], U8, name="v2_scale_rows", tag="slot_b", align_bytes=64)
-        w_rows = keep.tile([BLOCKS, W_PLANES, N], U8, name="w_rows", tag="slot_c", align_bytes=64)
+        list1 = keep.tile([P, J // STRIPE], U16, name="list1")
+        list2 = keep.tile([P, J // STRIPE], U16, name="list2")
+        v_scale_rows = keep.tile([P, T], U8, name="v_scale_rows", align_bytes=64)
+        v2_scale_rows = keep.tile([P, T], U8, name="v2_scale_rows", align_bytes=64)
+        w_rows = keep.tile([BLOCKS, W_PLANES, N], U8, name="w_rows", align_bytes=64)
         wv_w = keep.tile([P, 2, 2 * N], U8, name="wv_w", align_bytes=64)
-        v2_words = keep.tile([P, T], U32, name="v2_words", tag="slot_e", align_bytes=64)
-        picked_rows = keep.tile([P, 2, J], U8, name="picked_rows", tag="slot_f", align_bytes=64)
+        v2_words = keep.tile([P, T], U32, name="v2_words", align_bytes=64)
+        picked_rows = keep.tile([P, 2, J], U8, name="picked_rows", align_bytes=64)
         w_planes = keep.tile([P, W_PLANES, N], U8, name="w_planes", align_bytes=64)
         wt_plane = keep.tile([P, N], U8, name="wt_plane", align_bytes=64)
         b_rows = keep.tile([P, P], F32, name="b_rows")
@@ -56,24 +57,21 @@ def tile_list_gmu_relu_gate_kernel(
         b_neg = keep.tile([P, N // P], F32, name="b_neg")
         picked_planes = keep.tile([P, 2, 2 * J], U8, name="picked_planes", align_bytes=64)
         picked_v = [keep.tile([P, 2, HALF], U16, name="picked_v%d" % h, align_bytes=64) for h in range(2)]
-        v_words = keep.tile([P, T], U32, name="v_words", tag="slot_g", align_bytes=64)
+        v_words = keep.tile([P, T], U32, name="v_words", align_bytes=64)
         zt_w = keep.tile([P, 2 * N], U8, name="zt_w", align_bytes=64)
 
-        warm = keep.tile([P, 2], F32, name="warm")
-        nc.vector.memset(warm[:, 0:1], 0.0)
-        nc.vector.memset(v_scale_rows[0:V_ROWS, :].bitcast(I32), 0)
+        nc.vector.memset(v_scale_rows[0:SCALE_ROWS, :].bitcast(I32), 0)
         nc.vector.memset(w_planes[:].bitcast(I32), 0)
         nc.vector.memset(picked_planes[:].bitcast(I32), 0)
 
         nc.gpsimd.memset(v2_scale_rows[:].bitcast(I32), 0)
-        nc.scalar.dma_start(v2_scale_rows[V_ROWS:P:2, :].bitcast(I32), tab2_scales[0].bitcast(I32))
-        nc.scalar.activation(warm[:, 1:2], warm[:, 0:1], ACT.Sigmoid)
+        nc.scalar.dma_start(v2_scale_rows[SCALE_ROWS:P:2, :].bitcast(I32), tab2_scales[0].bitcast(I32))
         nc.gpsimd.memset(b_rows[:], 0.0)
         nc.gpsimd.dma_start(b_rows[0 : N // P, :], b.rearrange("(c p) -> c p", p=P))
         make_identity(nc, ident[:])
 
         nc.sync.dma_start(list1[:], offs)
-        nc.sync.dma_start(v_scale_rows[V_ROWS:P, :].bitcast(I32), tab_scales.rearrange("a q t -> q a t").bitcast(I32))
+        nc.sync.dma_start(v_scale_rows[SCALE_ROWS:P, :].bitcast(I32), tab_scales.rearrange("a q t -> q a t").bitcast(I32))
         nc.sync.dma_start(list2[:], offs2)
         nc.sync.dma_start(w_rows[:, ZV_PLANE:ZT_PLANE, :].bitcast(I32), zv_scales.rearrange("a q n -> q a n").bitcast(I32))
         nc.sync.dma_start(w_rows[:, ZT_PLANE, :].bitcast(I32), zt_scales[0].bitcast(I32))
@@ -83,69 +81,66 @@ def tile_list_gmu_relu_gate_kernel(
         nc.sync.dma_start(zt_w[:].bitcast(I32), zt_words[0].bitcast(I32))
         nc.sync.dma_start(wv_w[:].bitcast(I32), wv_words.rearrange("a p m -> p a m").bitcast(I32))
 
-        for r in range(4):
-            nc.scalar.dma_start(w_planes[r:P:QUAD, :, :].bitcast(I32), w_rows[r:BLOCKS:4, :, :].bitcast(I32))
+        for r in range(LIVE):
+            nc.scalar.dma_start(w_planes[r:P:QUAD, :, :].bitcast(I32), w_rows[r:BLOCKS:LIVE, :, :].bitcast(I32))
 
         nc.vector.tensor_copy(picked_rows[:, 0, :], v_scale_rows[:].indirect(list1[:]))
-        zv_w = keep.tile([P, 2, N], U32, name="zv_w", tag="slot_a", align_bytes=64)
+        zv_w = keep.tile([P, 2, N], U32, name="zv_w", tag="v_scale_rows", align_bytes=64)
         nc.sync.dma_start(zv_w[:].bitcast(I32), zv_words.rearrange("a p n c -> p a (n c)").bitcast(I32))
         nc.vector.tensor_copy(picked_rows[:, 1, :], v2_scale_rows[:].indirect(list2[:]))
-        for quad in range(4):
-            first = V_ROWS + 8 * quad
+        for quad in range(P // QUAD):
+            first = SCALE_ROWS + 2 * LIVE * quad
             nc.sync.dma_start(
-                picked_planes[QUAD * quad : QUAD * quad + 4, :, :].bitcast(I32),
-                picked_rows[first : first + 8, :, :].rearrange("p s j -> p (s j)").bitcast(I32),
+                picked_planes[QUAD * quad : QUAD * quad + LIVE, :, :].bitcast(I32),
+                picked_rows[first : first + 2 * LIVE, :, :].rearrange("p s j -> p (s j)").bitcast(I32),
             )
-        wt_raw = keep.tile([P, PACK, N], F32, name="wt_raw", tag="slot_c", align_bytes=64)
+        wt_raw = keep.tile([P, PACK, N], F32, name="wt_raw", tag="w_rows", align_bytes=64)
         nc.sync.dma_start(wt_raw[:], wt.rearrange("(p j) n -> p j n", j=PACK))
 
-        g_tiles = {}
-
-        def load_g(i, slot):
-            g_tiles[i] = keep.tile([P, T], F32, name="g%d" % i, tag=slot, align_bytes=64)
-            nc.sync.dma_start(g_tiles[i][:], gT[P * i : P * (i + 1), :])
+        def entries(list_tile, start, stop):
+            return list_tile[:, start // STRIPE : stop // STRIPE]
 
         def gather_words(h, v2_out, pairs):
-            cols = slice(h * HALF_COLS, (h + 1) * HALF_COLS)
-            nc.vector.tensor_copy(v2_out, v2_words[:].indirect(list2[:, cols]))
-            nc.vector.tensor_copy(pairs, v_words[:].indirect(list1[:, cols]))
+            nc.vector.tensor_copy(v2_out, v2_words[:].indirect(entries(list2, h * HALF, (h + 1) * HALF)))
+            nc.vector.tensor_copy(pairs, v_words[:].indirect(entries(list1, h * HALF, (h + 1) * HALF)))
             nc.vector.tensor_copy(picked_v[h][:], pairs.bitcast(U16).rearrange("p (t d) -> p d t", d=2))
 
-        first_v2 = keep.tile([P, HALF], U32, name="first_v2", tag="slot_b", align_bytes=64)
-        first_pairs = keep.tile([P, HALF], U32, name="first_pairs", tag="slot_d", align_bytes=64)
+        first_v2 = keep.tile([P, HALF], U32, name="first_v2", tag="v2_scale_rows", align_bytes=64)
+        first_pairs = keep.tile([P, HALF], U32, name="first_pairs", align_bytes=64)
         gather_words(0, first_v2[:], first_pairs[:])
-        second_words = keep.tile([P, 2, HALF], U32, name="second_words", tag="slot_d", align_bytes=64)
+        second_words = keep.tile([P, 2, HALF], U32, name="second_words", tag="first_pairs", align_bytes=64)
         gather_words(1, second_words[:, 0, :], second_words[:, 1, :])
         picked_v2 = [first_v2[:], second_words[:, 0, :]]
 
         wt_words = keep.tile([P, N], U32, name="wt_words", align_bytes=64)
-        for h in range(2):
-            cut = slice(h * N // 2, (h + 1) * N // 2)
-            wt_bf = keep.tile([P, N // 2, PACK], BF16, name="wt_bf%d" % h, align_bytes=64)
+        for c in range(2):
+            cut = slice(c * N // 2, (c + 1) * N // 2)
+            wt_bf = keep.tile([P, N // 2, PACK], BF16, name="wt_bf%d" % c, align_bytes=64)
             nc.scalar.copy(wt_bf[:], wt_raw[:, :, cut].rearrange("p j n -> p n j"))
             nc.vector.quantize_mx(
                 wt_words[:, cut].bitcast(FP8X4), wt_plane[:, cut], wt_bf[:].rearrange("p n j -> p (n j)")
             )
 
-        for i, slot in enumerate(("slot_f", "slot_e", "slot_g", "slot_c")):
-            load_g(i, slot)
+        g_tiles = []
+        for i, tag in enumerate(("picked_rows", "v2_words", "v_words", "w_rows")):
+            g_tiles.append(keep.tile([P, T], F32, name="g%d" % i, tag=tag, align_bytes=64))
+            nc.sync.dma_start(g_tiles[i][:], gT[P * i : P * (i + 1), :])
 
-        b_turned = psum.tile([P, HALF], F32, name="b_turned", tag="hv", bufs=3)
+        b_turned = psum.tile([P, HALF], F32, name="b_turned", tag="hv", bufs=H_BANKS)
         nc.tensor.transpose(b_turned[:, 0:P], b_rows[:], ident[:])
-        nc.scalar.copy(b_pos[:], b_turned[:, 0 : N // P])
-        nc.scalar.activation(b_neg[:], b_turned[:, 0 : N // P], ACT.Copy, scale=-1.0)
+        nc.vector.tensor_copy(b_pos[:], b_turned[:, 0 : N // P])
+        nc.vector.tensor_scalar_mul(b_neg[:], b_turned[:, 0 : N // P], -1.0)
 
         def products(unit, i, h):
             n_cols = slice(P * i, P * (i + 1))
             n_bytes = slice(2 * P * i, 2 * P * (i + 1))
-            j_cols = slice(HALF * h, HALF * (h + 1))
             v_codes = [picked_v[h][:, a, :].bitcast(FP4X4) for a in range(2)]
-            v_planes = [picked_planes[:, a, j_cols] for a in range(2)]
+            v_planes = [picked_planes[:, a, HALF * h : HALF * (h + 1)] for a in range(2)]
             v2_codes = picked_v2[h].bitcast(FP8X4)
             v2_plane = picked_planes[:, 0, J + HALF * h : J + HALF * (h + 1)]
-            z = psum.tile([P, HALF], F32, name="z", tag="z", bufs=2)
-            hv = psum.tile([P, HALF], F32, name="hv", tag="hv", bufs=3)
-            ht = psum.tile([P, HALF], F32, name="ht", tag="ht", bufs=3)
+            z = psum.tile([P, HALF], F32, name="z", bufs=Z_BANKS)
+            hv = psum.tile([P, HALF], F32, name="hv", bufs=H_BANKS)
+            ht = psum.tile([P, HALF], F32, name="ht", bufs=H_BANKS)
             nc.tensor.matmul_mx(
                 z[:], zt_w[:, n_bytes].bitcast(FP4X4), w_planes[:, ZT_PLANE, n_cols],
                 v2_codes, v2_plane, start=True, stop=False,
@@ -164,8 +159,8 @@ def tile_list_gmu_relu_gate_kernel(
                 ht[:], wt_words[:, n_cols].bitcast(FP8X4), wt_plane[:, n_cols],
                 v2_codes, v2_plane, start=True, stop=True,
             )
-            gate = keep.tile([P, HALF], F32, name="gate", tag="gate%d" % (unit % RING))
-            rest = keep.tile([P, HALF], F32, name="rest", tag="rest%d" % (unit % RING), align_bytes=64)
+            gate = keep.tile([P, HALF], F32, name="gate%d" % unit)
+            rest = keep.tile([P, HALF], F32, name="rest%d" % unit, align_bytes=64)
             nc.scalar.activation(gate[:], z[:], ACT.Sigmoid, bias=b_pos[:, i : i + 1])
             nc.scalar.activation(rest[:], z[:], ACT.Sigmoid, bias=b_neg[:, i : i + 1], scale=-1.0)
             nc.vector.scalar_tensor_tensor(part_v[:, unit, :], hv[:], 0.0, gate[:], ALU.max, ALU.mult)
@@ -175,51 +170,50 @@ def tile_list_gmu_relu_gate_kernel(
         part_v = keep.tile([P, len(units), HALF], F32, name="part_v")
         part_t = keep.tile([P, len(units), HALF], F32, name="part_t")
 
-        def listed_g(i, h, cut=slice(0, HALF)):
-            return g_tiles[i][:].indirect(list1[:, (h * HALF + cut.start) // 16 : (h * HALF + cut.stop) // 16])
+        def listed_g(i, h, cut):
+            return g_tiles[i][:].indirect(entries(list1, h * HALF + cut.start, h * HALF + cut.stop))
 
-        def store(i, h, res, cut=slice(0, HALF)):
-            nc.sync.dma_start(out[P * i : P * (i + 1), HALF * h + cut.start : HALF * h + cut.stop], res)
+        def store(i, h, cut, values):
+            nc.sync.dma_start(out[P * i : P * (i + 1), HALF * h + cut.start : HALF * h + cut.stop], values)
 
         def finish_on_gpsimd(unit):
             i, h = units[unit]
             factor = keep.tile([P, HALF], F32, name="factor", tag="rest%d" % (unit + 1), align_bytes=64)
-            nc.vector.tensor_copy(factor[:], listed_g(i, h))
+            nc.vector.tensor_copy(factor[:], listed_g(i, h, slice(0, HALF)))
             early = work.tile([P, HALF], F32, name="early")
             nc.gpsimd.tensor_tensor(early[:], part_v[:, unit, :], factor[:], ALU.mult)
-            store(i, h, early[:])
+            store(i, h, slice(0, HALF), early[:])
 
         for unit, (i, h) in enumerate(units):
             products(unit, i, h)
-            if 0 < unit <= GPSIMD_FINISHED:
+            if 0 < unit <= GPSIMD_FINISHES:
                 finish_on_gpsimd(unit - 1)
-            if unit < GPSIMD_UNITS:
+            if unit < GPSIMD_ADDS:
                 nc.gpsimd.tensor_tensor(part_v[:, unit, :], part_v[:, unit, :], part_t[:, unit, :], ALU.add)
 
-        totals = [part_v[:, unit, :] for unit in range(GPSIMD_UNITS)]
-        for unit in range(GPSIMD_UNITS, len(units)):
-            turned = psum.tile([P, HALF], F32, name="turned", tag="hv", bufs=3)
-            for c in range(HALF // P):
-                block = slice(P * c, P * (c + 1))
+        blocks = [slice(P * c, P * (c + 1)) for c in range(HALF // P)]
+        totals = [part_v[:, unit, :] for unit in range(GPSIMD_ADDS)]
+        for unit in range(GPSIMD_ADDS, len(units)):
+            turned = psum.tile([P, HALF], F32, name="turned", tag="hv", bufs=H_BANKS)
+            for block in blocks:
                 for part, first in ((part_v, True), (part_t, False)):
                     nc.tensor.matmul(
                         turned[:, block], part[:, unit, block], ident[:], start=first, stop=not first, is_transpose=True
                     )
             turned_sum = work.tile([P, HALF], F32, name="turned_sum")
             nc.scalar.copy(turned_sum[:], turned[:])
-            back = psum.tile([P, HALF], F32, name="back", tag="z", bufs=2)
-            for c in range(HALF // P):
-                block = slice(P * c, P * (c + 1))
+            back = psum.tile([P, HALF], F32, name="back", tag="z", bufs=Z_BANKS)
+            for block in blocks:
                 nc.tensor.transpose(back[:, block], turned_sum[:, block], ident[:])
-            total = work.tile([P, HALF], F32, name="total", bufs=len(units) - GPSIMD_UNITS)
+            total = work.tile([P, HALF], F32, name="total", bufs=len(units) - GPSIMD_ADDS)
             nc.scalar.copy(total[:], back[:])
             totals.append(total[:])
 
         res = keep.tile([P, len(units), HALF], F32, name="res", tag="rest%d" % (len(units) - 1), align_bytes=64)
-        for unit in range(GPSIMD_FINISHED, len(units)):
+        for unit in range(GPSIMD_FINISHES, len(units)):
             i, h = units[unit]
             pieces = 2 if unit == len(units) - 1 else 1
             for piece in range(pieces):
                 cut = slice(piece * HALF // pieces, (piece + 1) * HALF // pieces)
                 nc.vector.tensor_tensor(res[:, unit, cut], listed_g(i, h, cut), totals[unit][:, cut], ALU.mult)
-                store(i, h, res[:, unit, cut], cut)
+                store(i, h, cut, res[:, unit, cut])

@@ -26,6 +26,7 @@ QUAD = 32
 LIVE = 4
 SCALE_ROWS = P - 2 * BLOCKS
 ZV_PLANE, ZT_PLANE, WV_PLANE, W_PLANES = 0, 2, 3, 5
+WT_BF_AT, PAIRS_AT, V2_AT = 0, 1024, 2048
 Z_BANKS, H_BANKS = 2, 3
 GPSIMD_ADDS = 5
 GPSIMD_FINISHES = 2
@@ -38,6 +39,7 @@ def tile_list_gmu_relu_gate_kernel(
     nc = tc.nc
     with ExitStack() as ctx:
         keep = ctx.enter_context(tc.tile_pool(name="keep", bufs=1))
+        placed = ctx.enter_context(tc.tile_pool(name="placed", bufs=1))
         work = ctx.enter_context(tc.tile_pool(name="work", bufs=2))
         psum = ctx.enter_context(tc.psum_pool(name="psum", bufs=1))
 
@@ -100,29 +102,36 @@ def tile_list_gmu_relu_gate_kernel(
         def entries(list_tile, start, stop):
             return list_tile[:, start // STRIPE : stop // STRIPE]
 
-        def gather_words(h, v2_out, pairs):
-            nc.vector.tensor_copy(v2_out, v2_words[:].indirect(entries(list2, h * HALF, (h + 1) * HALF)))
-            nc.vector.tensor_copy(pairs, v_words[:].indirect(entries(list1, h * HALF, (h + 1) * HALF)))
-            nc.vector.tensor_copy(picked_v[h][:], pairs.bitcast(U16).rearrange("p (t d) -> p d t", d=2))
+        def gather_v(h):
+            pairs = placed.tile([P, HALF], U32, name="pairs%d" % h, offset=PAIRS_AT, align_bytes=64)
+            nc.vector.tensor_copy(pairs[:], v_words[:].indirect(entries(list1, h * HALF, (h + 1) * HALF)))
+            nc.vector.tensor_copy(picked_v[h][:], pairs[:].bitcast(U16).rearrange("p (t d) -> p d t", d=2))
 
-        first_v2 = keep.tile([P, HALF], U32, name="first_v2", tag="v2_scale_rows", align_bytes=64)
-        first_pairs = keep.tile([P, HALF], U32, name="first_pairs", align_bytes=64)
-        gather_words(0, first_v2[:], first_pairs[:])
-        second_words = keep.tile([P, 2, HALF], U32, name="second_words", tag="first_pairs", align_bytes=64)
-        gather_words(1, second_words[:, 0, :], second_words[:, 1, :])
-        picked_v2 = [first_v2[:], second_words[:, 0, :]]
+        def gather_v2(h, words):
+            nc.vector.tensor_copy(words[:], v2_words[:].indirect(entries(list2, h * HALF, (h + 1) * HALF)))
+            return words
+
+        picked_v2 = [gather_v2(0, keep.tile([P, HALF], U32, name="first_v2", tag="v2_scale_rows", align_bytes=64))]
+        gather_v(0)
+        gather_v(1)
+        picked_v2.append(gather_v2(1, placed.tile([P, HALF], U32, name="second_v2", offset=V2_AT, align_bytes=64)))
 
         wt_words = keep.tile([P, N], U32, name="wt_words", align_bytes=64)
-        for c in range(2):
-            cut = slice(c * N // 2, (c + 1) * N // 2)
-            wt_bf = keep.tile([P, N // 2, PACK], BF16, name="wt_bf%d" % c, align_bytes=64)
-            nc.scalar.copy(wt_bf[:], wt_raw[:, :, cut].rearrange("p j n -> p n j"))
+        cuts = [slice(0, N // 2), slice(N // 2, N)]
+        wt_bf = [
+            keep.tile([P, N // 2, PACK], BF16, name="wt_bf0", align_bytes=64),
+            placed.tile([P, N // 2, PACK], BF16, name="wt_bf1", offset=WT_BF_AT, align_bytes=64),
+        ]
+        woven = [wt_raw[:, :, cut].rearrange("p j n -> p n j") for cut in cuts]
+        nc.scalar.copy(wt_bf[0][:], woven[0])
+        nc.gpsimd.tensor_scalar(wt_bf[1][:], woven[1], 1.0, 0.0, ALU.mult, ALU.add)
+        for cut, rounded in zip(cuts, wt_bf):
             nc.vector.quantize_mx(
-                wt_words[:, cut].bitcast(FP8X4), wt_plane[:, cut], wt_bf[:].rearrange("p n j -> p (n j)")
+                wt_words[:, cut].bitcast(FP8X4), wt_plane[:, cut], rounded[:].rearrange("p n j -> p (n j)")
             )
 
         g_tiles = []
-        for i, tag in enumerate(("picked_rows", "v2_words", "v_words", "w_rows")):
+        for i, tag in enumerate(("picked_rows", "v_words", "v2_words", "w_rows")):
             g_tiles.append(keep.tile([P, T], F32, name="g%d" % i, tag=tag, align_bytes=64))
             nc.sync.dma_start(g_tiles[i][:], gT[P * i : P * (i + 1), :])
 
@@ -131,12 +140,12 @@ def tile_list_gmu_relu_gate_kernel(
         nc.vector.tensor_copy(b_pos[:], b_turned[:, 0 : N // P])
         nc.vector.tensor_scalar_mul(b_neg[:], b_turned[:, 0 : N // P], -1.0)
 
-        def products(unit, i, h):
+        def first_product(unit, i, h):
             n_cols = slice(P * i, P * (i + 1))
             n_bytes = slice(2 * P * i, 2 * P * (i + 1))
             v_codes = [picked_v[h][:, a, :].bitcast(FP4X4) for a in range(2)]
             v_planes = [picked_planes[:, a, HALF * h : HALF * (h + 1)] for a in range(2)]
-            v2_codes = picked_v2[h].bitcast(FP8X4)
+            v2_codes = picked_v2[h][:].bitcast(FP8X4)
             v2_plane = picked_planes[:, 0, J + HALF * h : J + HALF * (h + 1)]
             z = psum.tile([P, HALF], F32, name="z", bufs=Z_BANKS)
             hv = psum.tile([P, HALF], F32, name="hv", bufs=H_BANKS)
@@ -164,11 +173,19 @@ def tile_list_gmu_relu_gate_kernel(
             nc.scalar.activation(gate[:], z[:], ACT.Sigmoid, bias=b_pos[:, i : i + 1])
             nc.scalar.activation(rest[:], z[:], ACT.Sigmoid, bias=b_neg[:, i : i + 1], scale=-1.0)
             nc.vector.scalar_tensor_tensor(part_v[:, unit, :], hv[:], 0.0, gate[:], ALU.max, ALU.mult)
-            nc.vector.scalar_tensor_tensor(part_t[:, unit, :], ht[:], 0.0, rest[:], ALU.max, ALU.mult)
+            return ht, rest
+
+        def second_product(unit, tag):
+            ht, rest = pending[unit]
+            part_t.append(keep.tile([P, HALF], F32, name="part_t%d" % unit, tag=tag))
+            nc.vector.scalar_tensor_tensor(part_t[unit][:], ht[:], 0.0, rest[:], ALU.max, ALU.mult)
+            if unit < GPSIMD_ADDS:
+                nc.gpsimd.tensor_tensor(part_v[:, unit, :], part_v[:, unit, :], part_t[unit][:], ALU.add)
 
         units = [(i, h) for h in range(2) for i in range(N // P)]
         part_v = keep.tile([P, len(units), HALF], F32, name="part_v")
-        part_t = keep.tile([P, len(units), HALF], F32, name="part_t")
+        part_t = []
+        pending = []
 
         def listed_g(i, h, cut):
             return g_tiles[i][:].indirect(entries(list1, h * HALF + cut.start, h * HALF + cut.stop))
@@ -185,21 +202,21 @@ def tile_list_gmu_relu_gate_kernel(
             store(i, h, slice(0, HALF), early[:])
 
         for unit, (i, h) in enumerate(units):
-            products(unit, i, h)
+            pending.append(first_product(unit, i, h))
+            if unit == 1:
+                second_product(0, "gate1")
+            if unit > 0:
+                second_product(unit, "part_t%d" % unit)
             if 0 < unit <= GPSIMD_FINISHES:
                 finish_on_gpsimd(unit - 1)
-            if unit < GPSIMD_ADDS:
-                nc.gpsimd.tensor_tensor(part_v[:, unit, :], part_v[:, unit, :], part_t[:, unit, :], ALU.add)
 
         blocks = [slice(P * c, P * (c + 1)) for c in range(HALF // P)]
         totals = [part_v[:, unit, :] for unit in range(GPSIMD_ADDS)]
         for unit in range(GPSIMD_ADDS, len(units)):
             turned = psum.tile([P, HALF], F32, name="turned", tag="hv", bufs=H_BANKS)
             for block in blocks:
-                for part, first in ((part_v, True), (part_t, False)):
-                    nc.tensor.matmul(
-                        turned[:, block], part[:, unit, block], ident[:], start=first, stop=not first, is_transpose=True
-                    )
+                for part, first in ((part_v[:, unit, block], True), (part_t[unit][:, block], False)):
+                    nc.tensor.matmul(turned[:, block], part, ident[:], start=first, stop=not first, is_transpose=True)
             turned_sum = work.tile([P, HALF], F32, name="turned_sum")
             nc.scalar.copy(turned_sum[:], turned[:])
             back = psum.tile([P, HALF], F32, name="back", tag="z", bufs=Z_BANKS)

@@ -26,10 +26,14 @@ QUAD = 32
 LIVE = 4
 SCALE_ROWS = P - 2 * BLOCKS
 ZV_PLANE, ZT_PLANE, WV_PLANE, W_PLANES = 0, 2, 3, 5
-WT_BF_AT, PAIRS_AT, V2_AT = 0, 1024, 2048
+WT_G_AT, PAIRS_AT, V2_PICK1_AT = 0, 1024, 2048
+ZV_AT, V_ROWS_AT, ZT_AT = 4096, 8128, 8192
+B_RAW_AT, V2_PICK0_AT = 10240, 10240
+AV_AT, B_FIRST_AT, WT_S_AT = 16384, 18400, 18432
 Z_BANKS, H_BANKS = 2, 3
-GPSIMD_ADDS = 5
-GPSIMD_FINISHES = 2
+REST_UNITS, GPSIMD_ADDS, GPSIMD_FINISHES = (2,), 4, 2
+GATHER_AFTER = {1: 0, 2: 1}
+BACK_TAG, BACK_BUFS, RES_AFTER = "ht", 3, 7
 
 
 def tile_list_gmu_relu_gate_kernel(
@@ -45,50 +49,50 @@ def tile_list_gmu_relu_gate_kernel(
 
         list1 = keep.tile([P, J // STRIPE], U16, name="list1")
         list2 = keep.tile([P, J // STRIPE], U16, name="list2")
-        v_scale_rows = keep.tile([P, T], U8, name="v_scale_rows", align_bytes=64)
+        v_scale_rows = placed.tile([P, T], U8, name="v_scale_rows", offset=V_ROWS_AT, align_bytes=64)
         v2_scale_rows = keep.tile([P, T], U8, name="v2_scale_rows", align_bytes=64)
         w_rows = keep.tile([BLOCKS, W_PLANES, N], U8, name="w_rows", align_bytes=64)
         wv_w = keep.tile([P, 2, 2 * N], U8, name="wv_w", align_bytes=64)
-        v2_words = keep.tile([P, T], U32, name="v2_words", align_bytes=64)
         picked_rows = keep.tile([P, 2, J], U8, name="picked_rows", align_bytes=64)
         w_planes = keep.tile([P, W_PLANES, N], U8, name="w_planes", align_bytes=64)
         wt_plane = keep.tile([P, N], U8, name="wt_plane", align_bytes=64)
+        b_pos = keep.tile([P, N // P], F32, name="b_pos")
         b_rows = keep.tile([P, P], F32, name="b_rows")
         ident = keep.tile([P, P], F32, name="ident")
-        b_pos = keep.tile([P, N // P], F32, name="b_pos")
         b_neg = keep.tile([P, N // P], F32, name="b_neg")
         picked_planes = keep.tile([P, 2, 2 * J], U8, name="picked_planes", align_bytes=64)
         picked_v = [keep.tile([P, 2, HALF], U16, name="picked_v%d" % h, align_bytes=64) for h in range(2)]
         v_words = keep.tile([P, T], U32, name="v_words", align_bytes=64)
-        zt_w = keep.tile([P, 2 * N], U8, name="zt_w", align_bytes=64)
+        v2_words = keep.tile([P, T], U32, name="v2_words", align_bytes=64)
 
+        nc.gpsimd.memset(v2_scale_rows[:].bitcast(I32), 0)
         nc.vector.memset(v_scale_rows[0:SCALE_ROWS, :].bitcast(I32), 0)
         nc.vector.memset(w_planes[:].bitcast(I32), 0)
         nc.vector.memset(picked_planes[:].bitcast(I32), 0)
 
-        nc.gpsimd.memset(v2_scale_rows[:].bitcast(I32), 0)
-        nc.scalar.dma_start(v2_scale_rows[SCALE_ROWS:P:2, :].bitcast(I32), tab2_scales[0].bitcast(I32))
         nc.gpsimd.memset(b_rows[:], 0.0)
         nc.gpsimd.dma_start(b_rows[0 : N // P, :], b.rearrange("(c p) -> c p", p=P))
         make_identity(nc, ident[:])
 
+        nc.scalar.dma_start(v2_scale_rows[SCALE_ROWS:P:2, :].bitcast(I32), tab2_scales[0].bitcast(I32))
         nc.sync.dma_start(list1[:], offs)
         nc.sync.dma_start(v_scale_rows[SCALE_ROWS:P, :].bitcast(I32), tab_scales.rearrange("a q t -> q a t").bitcast(I32))
         nc.sync.dma_start(list2[:], offs2)
+        nc.sync.dma_start(w_rows[:, WV_PLANE:W_PLANES, :].bitcast(I32), wv_scales.rearrange("a q n -> q a n").bitcast(I32))
         nc.sync.dma_start(w_rows[:, ZV_PLANE:ZT_PLANE, :].bitcast(I32), zv_scales.rearrange("a q n -> q a n").bitcast(I32))
         nc.sync.dma_start(w_rows[:, ZT_PLANE, :].bitcast(I32), zt_scales[0].bitcast(I32))
-        nc.sync.dma_start(w_rows[:, WV_PLANE:W_PLANES, :].bitcast(I32), wv_scales.rearrange("a q n -> q a n").bitcast(I32))
         nc.sync.dma_start(v2_words[:].bitcast(I32), tab2_words[0].rearrange("p t c -> p (t c)").bitcast(I32))
-        nc.sync.dma_start(v_words[:].bitcast(I32), tab_words[0].rearrange("p t c -> p (t c)").bitcast(I32))
-        nc.sync.dma_start(zt_w[:].bitcast(I32), zt_words[0].bitcast(I32))
         nc.sync.dma_start(wv_w[:].bitcast(I32), wv_words.rearrange("a p m -> p a m").bitcast(I32))
+        nc.sync.dma_start(v_words[:].bitcast(I32), tab_words[0].rearrange("p t c -> p (t c)").bitcast(I32))
 
         for r in range(LIVE):
             nc.scalar.dma_start(w_planes[r:P:QUAD, :, :].bitcast(I32), w_rows[r:BLOCKS:LIVE, :, :].bitcast(I32))
 
         nc.vector.tensor_copy(picked_rows[:, 0, :], v_scale_rows[:].indirect(list1[:]))
-        zv_w = keep.tile([P, 2, N], U32, name="zv_w", tag="v_scale_rows", align_bytes=64)
+        zv_w = placed.tile([P, 2, N], U32, name="zv_w", offset=ZV_AT, align_bytes=64)
+        zt_w = placed.tile([P, 2 * N], U8, name="zt_w", offset=ZT_AT, align_bytes=64)
         nc.sync.dma_start(zv_w[:].bitcast(I32), zv_words.rearrange("a p n c -> p a (n c)").bitcast(I32))
+        nc.sync.dma_start(zt_w[:].bitcast(I32), zt_words[0].bitcast(I32))
         nc.vector.tensor_copy(picked_rows[:, 1, :], v2_scale_rows[:].indirect(list2[:]))
         for quad in range(P // QUAD):
             first = SCALE_ROWS + 2 * LIVE * quad
@@ -96,96 +100,89 @@ def tile_list_gmu_relu_gate_kernel(
                 picked_planes[QUAD * quad : QUAD * quad + LIVE, :, :].bitcast(I32),
                 picked_rows[first : first + 2 * LIVE, :, :].rearrange("p s j -> p (s j)").bitcast(I32),
             )
-        wt_raw = keep.tile([P, PACK, N], F32, name="wt_raw", tag="w_rows", align_bytes=64)
+        wt_raw = keep.tile([P, PACK, N], F32, name="wt_raw", tag="v2_scale_rows", align_bytes=64)
         nc.sync.dma_start(wt_raw[:], wt.rearrange("(p j) n -> p j n", j=PACK))
 
         def entries(list_tile, start, stop):
             return list_tile[:, start // STRIPE : stop // STRIPE]
 
+        def gather(picked, window, list_tile, h):
+            nc.vector.tensor_copy(picked[:], window[:].indirect(entries(list_tile, h * HALF, (h + 1) * HALF)))
+            return picked
+
         def gather_v(h):
             pairs = placed.tile([P, HALF], U32, name="pairs%d" % h, offset=PAIRS_AT, align_bytes=64)
-            nc.vector.tensor_copy(pairs[:], v_words[:].indirect(entries(list1, h * HALF, (h + 1) * HALF)))
+            gather(pairs, v_words, list1, h)
             nc.vector.tensor_copy(picked_v[h][:], pairs[:].bitcast(U16).rearrange("p (t d) -> p d t", d=2))
 
-        def gather_v2(h, words):
-            nc.vector.tensor_copy(words[:], v2_words[:].indirect(entries(list2, h * HALF, (h + 1) * HALF)))
-            return words
-
-        picked_v2 = [gather_v2(0, keep.tile([P, HALF], U32, name="first_v2", tag="v2_scale_rows", align_bytes=64))]
+        picked_v2 = [gather(placed.tile([P, HALF], U32, name="first_v2", offset=V2_PICK0_AT, align_bytes=64), v2_words, list2, 0)]
         gather_v(0)
         gather_v(1)
-        picked_v2.append(gather_v2(1, placed.tile([P, HALF], U32, name="second_v2", offset=V2_AT, align_bytes=64)))
-
-        wt_words = keep.tile([P, N], U32, name="wt_words", align_bytes=64)
-        cuts = [slice(0, N // 2), slice(N // 2, N)]
-        wt_bf = [
-            keep.tile([P, N // 2, PACK], BF16, name="wt_bf0", align_bytes=64),
-            placed.tile([P, N // 2, PACK], BF16, name="wt_bf1", offset=WT_BF_AT, align_bytes=64),
-        ]
-        woven = [wt_raw[:, :, cut].rearrange("p j n -> p n j") for cut in cuts]
-        nc.scalar.copy(wt_bf[0][:], woven[0])
-        nc.gpsimd.tensor_scalar(wt_bf[1][:], woven[1], 1.0, 0.0, ALU.mult, ALU.add)
-        for cut, rounded in zip(cuts, wt_bf):
-            nc.vector.quantize_mx(
-                wt_words[:, cut].bitcast(FP8X4), wt_plane[:, cut], rounded[:].rearrange("p n j -> p (n j)")
-            )
-
-        g_tiles = []
-        for i, tag in enumerate(("picked_rows", "v_words", "v2_words", "w_rows")):
-            g_tiles.append(keep.tile([P, T], F32, name="g%d" % i, tag=tag, align_bytes=64))
-            nc.sync.dma_start(g_tiles[i][:], gT[P * i : P * (i + 1), :])
-
+        picked_v2.append(
+            gather(placed.tile([P, HALF], U32, name="second_v2", offset=V2_PICK1_AT, align_bytes=64), v2_words, list2, 1)
+        )
         b_turned = psum.tile([P, HALF], F32, name="b_turned", tag="hv", bufs=H_BANKS)
         nc.tensor.transpose(b_turned[:, 0:P], b_rows[:], ident[:])
         nc.vector.tensor_copy(b_pos[:], b_turned[:, 0 : N // P])
         nc.vector.tensor_scalar_mul(b_neg[:], b_turned[:, 0 : N // P], -1.0)
-
-        def first_product(unit, i, h):
-            n_cols = slice(P * i, P * (i + 1))
-            n_bytes = slice(2 * P * i, 2 * P * (i + 1))
-            v_codes = [picked_v[h][:, a, :].bitcast(FP4X4) for a in range(2)]
-            v_planes = [picked_planes[:, a, HALF * h : HALF * (h + 1)] for a in range(2)]
-            v2_codes = picked_v2[h][:].bitcast(FP8X4)
-            v2_plane = picked_planes[:, 0, J + HALF * h : J + HALF * (h + 1)]
-            z = psum.tile([P, HALF], F32, name="z", bufs=Z_BANKS)
-            hv = psum.tile([P, HALF], F32, name="hv", bufs=H_BANKS)
-            ht = psum.tile([P, HALF], F32, name="ht", bufs=H_BANKS)
-            nc.tensor.matmul_mx(
-                z[:], zt_w[:, n_bytes].bitcast(FP4X4), w_planes[:, ZT_PLANE, n_cols],
-                v2_codes, v2_plane, start=True, stop=False,
-            )
-            for a in range(2):
-                nc.tensor.matmul_mx(
-                    z[:], zv_w[:, a, n_cols].bitcast(FP8X4), w_planes[:, ZV_PLANE + a, n_cols],
-                    v_codes[a], v_planes[a], start=False, stop=(a == 1),
-                )
-            for a in range(2):
-                nc.tensor.matmul_mx(
-                    hv[:], wv_w[:, a, n_bytes].bitcast(FP4X4), w_planes[:, WV_PLANE + a, n_cols],
-                    v_codes[a], v_planes[a], start=(a == 0), stop=(a == 1),
-                )
-            nc.tensor.matmul_mx(
-                ht[:], wt_words[:, n_cols].bitcast(FP8X4), wt_plane[:, n_cols],
-                v2_codes, v2_plane, start=True, stop=True,
-            )
-            gate = keep.tile([P, HALF], F32, name="gate%d" % unit)
-            rest = keep.tile([P, HALF], F32, name="rest%d" % unit, align_bytes=64)
-            nc.scalar.activation(gate[:], z[:], ACT.Sigmoid, bias=b_pos[:, i : i + 1])
-            nc.scalar.activation(rest[:], z[:], ACT.Sigmoid, bias=b_neg[:, i : i + 1], scale=-1.0)
-            nc.vector.scalar_tensor_tensor(part_v[:, unit, :], hv[:], 0.0, gate[:], ALU.max, ALU.mult)
-            return ht, rest
-
-        def second_product(unit, tag):
-            ht, rest = pending[unit]
-            part_t.append(keep.tile([P, HALF], F32, name="part_t%d" % unit, tag=tag))
-            nc.vector.scalar_tensor_tensor(part_t[unit][:], ht[:], 0.0, rest[:], ALU.max, ALU.mult)
-            if unit < GPSIMD_ADDS:
-                nc.gpsimd.tensor_tensor(part_v[:, unit, :], part_v[:, unit, :], part_t[unit][:], ALU.add)
+        v2_planes = [picked_planes[:, 0, J + HALF * h : J + HALF * (h + 1)] for h in range(2)]
 
         units = [(i, h) for h in range(2) for i in range(N // P)]
+        wt_words = keep.tile([P, N], U32, name="wt_words", align_bytes=64)
         part_v = keep.tile([P, len(units), HALF], F32, name="part_v")
-        part_t = []
-        pending = []
+
+        def v_passes(bank, weight_of, plane, unit, start):
+            i, h = units[unit]
+            for a in range(2):
+                nc.tensor.matmul_mx(
+                    bank[:], weight_of(a, i), w_planes[:, plane + a, P * i : P * (i + 1)],
+                    picked_v[h][:, a, :].bitcast(FP4X4), picked_planes[:, a, HALF * h : HALF * (h + 1)],
+                    start=(start and a == 0), stop=(a == 1),
+                )
+
+        def v2_pass(bank, weight, weight_plane, unit, stop):
+            h = units[unit][1]
+            nc.tensor.matmul_mx(
+                bank[:], weight, weight_plane, picked_v2[h][:].bitcast(FP8X4), v2_planes[h], start=True, stop=stop
+            )
+
+        def make_hv(unit):
+            hv = psum.tile([P, HALF], F32, name="hv", bufs=H_BANKS)
+            v_passes(hv, lambda a, i: wv_w[:, a, 2 * P * i : 2 * P * (i + 1)].bitcast(FP4X4), WV_PLANE, unit, True)
+            return hv
+
+        def make_z(unit):
+            i = units[unit][0]
+            z = psum.tile([P, HALF], F32, name="z", bufs=Z_BANKS)
+            v2_pass(z, zt_w[:, 2 * P * i : 2 * P * (i + 1)].bitcast(FP4X4), w_planes[:, ZT_PLANE, P * i : P * (i + 1)], unit, False)
+            v_passes(z, lambda a, i: zv_w[:, a, P * i : P * (i + 1)].bitcast(FP8X4), ZV_PLANE, unit, False)
+            return z
+
+        def make_ht(unit):
+            i = units[unit][0]
+            ht = psum.tile([P, HALF], F32, name="ht", bufs=H_BANKS)
+            v2_pass(ht, wt_words[:, P * i : P * (i + 1)].bitcast(FP8X4), wt_plane[:, P * i : P * (i + 1)], unit, True)
+            return ht
+
+        def make_rest(unit, z):
+            i = units[unit][0]
+            rest = keep.tile([P, HALF], F32, name="rest%d" % unit, align_bytes=64)
+            nc.scalar.activation(rest[:], z[:], ACT.Sigmoid, bias=b_neg[:, i : i + 1], scale=-1.0)
+            return rest
+
+        def quantise_wt():
+            cuts = [slice(0, N // 2), slice(N // 2, N)]
+            wt_bf = [
+                placed.tile([P, N // 2, PACK], BF16, name="wt_bf0", offset=WT_G_AT, align_bytes=64),
+                placed.tile([P, N // 2, PACK], BF16, name="wt_bf1", offset=WT_S_AT, align_bytes=64),
+            ]
+            woven = [wt_raw[:, :, cut].rearrange("p j n -> p n j") for cut in cuts]
+            nc.gpsimd.tensor_scalar(wt_bf[0][:], woven[0], 1.0, 0.0, ALU.mult, ALU.add)
+            nc.scalar.copy(wt_bf[1][:], woven[1])
+            for cut, rounded in zip(cuts, wt_bf):
+                nc.vector.quantize_mx(
+                    wt_words[:, cut].bitcast(FP8X4), wt_plane[:, cut], rounded[:].rearrange("p n j -> p (n j)")
+                )
 
         def listed_g(i, h, cut):
             return g_tiles[i][:].indirect(entries(list1, h * HALF + cut.start, h * HALF + cut.stop))
@@ -193,44 +190,111 @@ def tile_list_gmu_relu_gate_kernel(
         def store(i, h, cut, values):
             nc.sync.dma_start(out[P * i : P * (i + 1), HALF * h + cut.start : HALF * h + cut.stop], values)
 
-        def finish_on_gpsimd(unit):
+        def plain_factor(unit, tag):
             i, h = units[unit]
-            factor = keep.tile([P, HALF], F32, name="factor", tag="rest%d" % (unit + 1), align_bytes=64)
+            factor = keep.tile([P, HALF], F32, name="factor%d" % unit, tag=tag, align_bytes=64)
             nc.vector.tensor_copy(factor[:], listed_g(i, h, slice(0, HALF)))
+            return factor
+
+        g_tiles = []
+        for i, tag in enumerate(("picked_rows", "v_words", "v2_words", "v2_scale_rows")):
+            g_tiles.append(keep.tile([P, T], F32, name="g%d" % i, tag=tag, align_bytes=64))
+            nc.sync.dma_start(g_tiles[i][:], gT[P * i : P * (i + 1), :])
+
+        def finish_on_gpsimd(unit, tag):
+            i, h = units[unit]
+            factor = plain_factor(unit, tag)
             early = work.tile([P, HALF], F32, name="early")
             nc.gpsimd.tensor_tensor(early[:], part_v[:, unit, :], factor[:], ALU.mult)
             store(i, h, slice(0, HALF), early[:])
 
-        for unit, (i, h) in enumerate(units):
-            pending.append(first_product(unit, i, h))
-            if unit == 1:
-                second_product(0, "gate1")
-            if unit > 0:
+        part_t, factors, pending = {}, {}, {}
+
+        def first_product(unit):
+            i = units[unit][0]
+            z = make_z(unit)
+            hv = make_hv(unit)
+            gate = keep.tile([P, HALF], F32, name="gate%d" % unit, align_bytes=64)
+            bias = b_pos[:, i : i + 1]
+            nc.scalar.activation(gate[:], z[:], ACT.Sigmoid, bias=bias)
+            pending[unit] = make_rest(unit, z)
+            nc.vector.scalar_tensor_tensor(part_v[:, unit, :], hv[:], 0.0, gate[:], ALU.max, ALU.mult)
+
+        def second_product(unit, tag):
+            part_t[unit] = keep.tile([P, HALF], F32, name="part_t%d" % unit, tag=tag, align_bytes=64)
+            nc.vector.scalar_tensor_tensor(part_t[unit][:], make_ht(unit)[:], 0.0, pending[unit][:], ALU.max, ALU.mult)
+
+        def rest_form(unit):
+            rest = make_rest(unit, make_z(unit))
+            part_t[unit] = keep.tile([P, HALF], F32, name="part_t%d" % unit, align_bytes=64)
+            nc.scalar.activation(part_t[unit][:], make_hv(unit)[:], ACT.Relu)
+            floor = keep.tile([P, 16], F32, name="floor%d" % unit, align_bytes=64)
+            nc.gpsimd.memset(floor[:, 0:1], 0.0)
+            nc.vector.scalar_tensor_tensor(
+                part_v[:, unit, :], make_ht(unit)[:], floor[:, 0:1], part_t[unit][:], ALU.max, ALU.subtract
+            )
+            nc.gpsimd.tensor_tensor(part_v[:, unit, :], part_v[:, unit, :], rest[:], ALU.mult)
+
+        def add_on_gpsimd(unit):
+            nc.gpsimd.tensor_tensor(part_v[:, unit, :], part_v[:, unit, :], part_t[unit][:], ALU.add)
+
+        first_product(0)
+        quantise_wt()
+        first_product(1)
+        second_product(0, "gate1")
+        add_on_gpsimd(0)
+        for unit in range(1, len(units)):
+            if unit in REST_UNITS:
+                rest_form(unit)
+            else:
+                if unit > 1:
+                    first_product(unit)
                 second_product(unit, "part_t%d" % unit)
-            if 0 < unit <= GPSIMD_FINISHES:
-                finish_on_gpsimd(unit - 1)
+            if unit < GPSIMD_ADDS:
+                add_on_gpsimd(unit)
+            if unit in GATHER_AFTER:
+                later = GATHER_AFTER[unit]
+                tag = ("floor%d" if unit in REST_UNITS else "rest%d") % unit
+                if later < GPSIMD_FINISHES:
+                    finish_on_gpsimd(later, tag)
+                else:
+                    factors[later] = plain_factor(later, tag)
 
         blocks = [slice(P * c, P * (c + 1)) for c in range(HALF // P)]
         totals = [part_v[:, unit, :] for unit in range(GPSIMD_ADDS)]
-        for unit in range(GPSIMD_ADDS, len(units)):
+
+        def turn(unit):
             turned = psum.tile([P, HALF], F32, name="turned", tag="hv", bufs=H_BANKS)
             for block in blocks:
-                for part, first in ((part_v[:, unit, block], True), (part_t[unit][:, block], False)):
-                    nc.tensor.matmul(turned[:, block], part, ident[:], start=first, stop=not first, is_transpose=True)
-            turned_sum = work.tile([P, HALF], F32, name="turned_sum")
+                for piece, first in ((part_v[:, unit, block], True), (part_t[unit][:, block], False)):
+                    nc.tensor.matmul(turned[:, block], piece, ident[:], start=first, stop=not first, is_transpose=True)
+            turned_sum = work.tile([P, HALF], F32, name="turned_sum", bufs=3)
             nc.scalar.copy(turned_sum[:], turned[:])
-            back = psum.tile([P, HALF], F32, name="back", tag="z", bufs=Z_BANKS)
+            return turned_sum
+
+        def turn_back(unit, turned_sum):
+            back = psum.tile([P, HALF], F32, name="back", tag=BACK_TAG, bufs=BACK_BUFS)
             for block in blocks:
                 nc.tensor.transpose(back[:, block], turned_sum[:, block], ident[:])
-            total = work.tile([P, HALF], F32, name="total", bufs=len(units) - GPSIMD_ADDS)
-            nc.scalar.copy(total[:], back[:])
-            totals.append(total[:])
+            if unit in factors:
+                totals.append(back[:])
+            else:
+                total = work.tile([P, HALF], F32, name="total", bufs=len(units) - GPSIMD_ADDS)
+                nc.scalar.copy(total[:], back[:])
+                totals.append(total[:])
 
-        res = keep.tile([P, len(units), HALF], F32, name="res", tag="rest%d" % (len(units) - 1), align_bytes=64)
+        waiting = turn(GPSIMD_ADDS)
+        for unit in range(GPSIMD_ADDS, len(units)):
+            ahead = turn(unit + 1) if unit + 1 < len(units) else None
+            turn_back(unit, waiting)
+            waiting = ahead
+
+        res = keep.tile([P, len(units), HALF], F32, name="res", tag="rest%d" % RES_AFTER, align_bytes=64)
         for unit in range(GPSIMD_FINISHES, len(units)):
             i, h = units[unit]
             pieces = 2 if unit == len(units) - 1 else 1
             for piece in range(pieces):
                 cut = slice(piece * HALF // pieces, (piece + 1) * HALF // pieces)
-                nc.vector.tensor_tensor(res[:, unit, cut], listed_g(i, h, cut), totals[unit][:, cut], ALU.mult)
+                factor = factors[unit][:, cut] if unit in factors else listed_g(i, h, cut)
+                nc.vector.tensor_tensor(res[:, unit, cut], factor, totals[unit][:, cut], ALU.mult)
                 store(i, h, cut, res[:, unit, cut])

@@ -238,6 +238,12 @@ def tile_list_gmu_relu_gate_kernel(
         def add_on_gpsimd(unit):
             nc.gpsimd.tensor_tensor(part_v[:, unit, :], part_v[:, unit, :], part_t[unit][:], ALU.add)
 
+        warm = psum.tile([P, HALF], F32, name="warm", tag="ht", bufs=H_BANKS)
+        for turn_number in range(3):
+            nc.tensor.matmul_mx(
+                warm[:], wv_w[:, 0, 0 : 2 * P].bitcast(FP4X4), w_planes[:, WV_PLANE, 0:P],
+                picked_v2[0][:].bitcast(FP8X4), w_planes[:, ZT_PLANE, :], start=True, stop=True,
+            )
         first_product(0)
         quantise_wt()
         first_product(1)

@@ -91,8 +91,8 @@ def tile_list_gmu_relu_gate_kernel(
         nc.vector.tensor_copy(picked_rows[:, 0, :], v_scale_rows[:].indirect(list1[:]))
         zv_w = placed.tile([P, 2, N], U32, name="zv_w", offset=ZV_AT, align_bytes=64)
         zt_w = placed.tile([P, 2 * N], U8, name="zt_w", offset=ZT_AT, align_bytes=64)
-        nc.sync.dma_start(zv_w[:].bitcast(I32), zv_words.rearrange("a p n c -> p a (n c)").bitcast(I32))
         nc.sync.dma_start(zt_w[:].bitcast(I32), zt_words[0].bitcast(I32))
+        nc.sync.dma_start(zv_w[:].bitcast(I32), zv_words.rearrange("a p n c -> p a (n c)").bitcast(I32))
         nc.vector.tensor_copy(picked_rows[:, 1, :], v2_scale_rows[:].indirect(list2[:]))
         for quad in range(P // QUAD):
             first = SCALE_ROWS + 2 * LIVE * quad
@@ -241,7 +241,7 @@ def tile_list_gmu_relu_gate_kernel(
         warm = psum.tile([P, HALF], F32, name="warm", tag="ht", bufs=H_BANKS)
         for turn_number in range(3):
             nc.tensor.matmul_mx(
-                warm[:], wv_w[:, 0, 0 : 2 * P].bitcast(FP4X4), w_planes[:, WV_PLANE, 0:P],
+                warm[:], zt_w[:, 0 : 2 * P].bitcast(FP4X4), w_planes[:, ZT_PLANE, 0:P],
                 picked_v2[0][:].bitcast(FP8X4), w_planes[:, ZT_PLANE, :], start=True, stop=True,
             )
         first_product(0)

@@ -65,14 +65,14 @@ def tile_list_gmu_relu_gate_kernel(
         v_words = keep.tile([P, T], U32, name="v_words", align_bytes=64)
         v2_words = keep.tile([P, T], U32, name="v2_words", align_bytes=64)
 
-        nc.gpsimd.memset(v2_scale_rows[:].bitcast(I32), 0)
+        nc.vector.memset(v2_scale_rows[:].bitcast(I32), 0)
         nc.vector.memset(v_scale_rows[0:SCALE_ROWS, :].bitcast(I32), 0)
-        nc.vector.memset(w_planes[:].bitcast(I32), 0)
-        nc.vector.memset(picked_planes[:].bitcast(I32), 0)
-
+        nc.gpsimd.memset(w_planes[:].bitcast(I32), 0)
         nc.gpsimd.memset(b_rows[:], 0.0)
         nc.gpsimd.dma_start(b_rows[0 : N // P, :], b.rearrange("(c p) -> c p", p=P))
         make_identity(nc, ident[:])
+        nc.gpsimd.memset(picked_planes[:, 0, :].bitcast(I32), 0)
+        nc.gpsimd.memset(picked_planes[:, 1, 0:J].bitcast(I32), 0)
 
         nc.scalar.dma_start(v2_scale_rows[SCALE_ROWS:P:2, :].bitcast(I32), tab2_scales[0].bitcast(I32))
         nc.sync.dma_start(list1[:], offs)

@@ -74,19 +74,23 @@ def tile_list_gmu_relu_gate_kernel(
         nc.gpsimd.memset(picked_planes[:, 0, :].bitcast(I32), 0)
         nc.gpsimd.memset(picked_planes[:, 1, 0:J].bitcast(I32), 0)
 
-        nc.scalar.dma_start(v2_scale_rows[SCALE_ROWS:P:2, :].bitcast(I32), tab2_scales[0].bitcast(I32))
+        def by_live_row(rows):
+            return rows.rearrange("(q r) t -> r q t", r=LIVE).bitcast(I32)
+
         nc.sync.dma_start(list1[:], offs)
-        nc.sync.dma_start(v_scale_rows[SCALE_ROWS:P, :].bitcast(I32), tab_scales.rearrange("a q t -> q a t").bitcast(I32))
-        nc.sync.dma_start(list2[:], offs2)
+        nc.sync.dma_start(v_scale_rows[SCALE_ROWS:P:2, :].bitcast(I32), by_live_row(tab_scales[0]))
+        nc.scalar.dma_start(v_scale_rows[SCALE_ROWS + 1 : P : 2, :].bitcast(I32), by_live_row(tab_scales[1]))
         nc.sync.dma_start(w_rows[:, WV_PLANE:W_PLANES, :].bitcast(I32), wv_scales.rearrange("a q n -> q a n").bitcast(I32))
-        nc.sync.dma_start(w_rows[:, ZV_PLANE:ZT_PLANE, :].bitcast(I32), zv_scales.rearrange("a q n -> q a n").bitcast(I32))
-        nc.sync.dma_start(w_rows[:, ZT_PLANE, :].bitcast(I32), zt_scales[0].bitcast(I32))
+        nc.scalar.dma_start(w_rows[:, ZV_PLANE:ZT_PLANE, :].bitcast(I32), zv_scales.rearrange("a q n -> q a n").bitcast(I32))
+        nc.scalar.dma_start(w_rows[:, ZT_PLANE, :].bitcast(I32), zt_scales[0].bitcast(I32))
+        nc.scalar.dma_start(v2_scale_rows[SCALE_ROWS:P:2, :].bitcast(I32), by_live_row(tab2_scales[0]))
         nc.sync.dma_start(v2_words[:].bitcast(I32), tab2_words[0].rearrange("p t c -> p (t c)").bitcast(I32))
+        nc.sync.dma_start(list2[:], offs2)
         nc.sync.dma_start(wv_w[:].bitcast(I32), wv_words.rearrange("a p m -> p a m").bitcast(I32))
         nc.sync.dma_start(v_words[:].bitcast(I32), tab_words[0].rearrange("p t c -> p (t c)").bitcast(I32))
 
         for r in range(LIVE):
-            nc.scalar.dma_start(w_planes[r:P:QUAD, :, :].bitcast(I32), w_rows[r:BLOCKS:LIVE, :, :].bitcast(I32))
+            nc.sync.dma_start(w_planes[r:P:QUAD, :, :].bitcast(I32), w_rows[r:BLOCKS:LIVE, :, :].bitcast(I32))
 
         nc.vector.tensor_copy(picked_rows[:, 0, :], v_scale_rows[:].indirect(list1[:]))
         zv_w = placed.tile([P, 2, N], U32, name="zv_w", offset=ZV_AT, align_bytes=64)
@@ -94,10 +98,10 @@ def tile_list_gmu_relu_gate_kernel(
         nc.sync.dma_start(zt_w[:].bitcast(I32), zt_words[0].bitcast(I32))
         nc.sync.dma_start(zv_w[:].bitcast(I32), zv_words.rearrange("a p n c -> p a (n c)").bitcast(I32))
         nc.vector.tensor_copy(picked_rows[:, 1, :], v2_scale_rows[:].indirect(list2[:]))
-        for quad in range(P // QUAD):
-            first = SCALE_ROWS + 2 * LIVE * quad
+        for r in range(LIVE):
+            first = SCALE_ROWS + 2 * LIVE * r
             nc.sync.dma_start(
-                picked_planes[QUAD * quad : QUAD * quad + LIVE, :, :].bitcast(I32),
+                picked_planes[r:P:QUAD, :, :].bitcast(I32),
                 picked_rows[first : first + 2 * LIVE, :, :].rearrange("p s j -> p (s j)").bitcast(I32),
             )
         wt_raw = keep.tile([P, PACK, N], F32, name="wt_raw", tag="v2_scale_rows", align_bytes=64)

@@ -29,7 +29,9 @@ ZV_PLANE, ZT_PLANE, WV_PLANE, W_PLANES = 0, 2, 3, 5
 WT_G_AT, PAIRS_AT, V2_PICK1_AT = 0, 1024, 2048
 ZV_AT, V_ROWS_AT, ZT_AT = 4096, 8128, 8192
 B_RAW_AT, V2_PICK0_AT = 10240, 10240
-AV_AT, B_FIRST_AT, WT_S_AT = 16384, 18400, 18432
+WT_S_AT = 18432
+WV_AT, V2_ROWS_AT, WT_AT = 20480, 22464, 24448
+B_POS_AT, B_NEG_AT = 22528, 22592
 Z_BANKS, H_BANKS = 2, 3
 REST_UNITS, GPSIMD_ADDS, GPSIMD_FINISHES = (2,), 4, 2
 GATHER_AFTER = {1: 0, 2: 1}
@@ -50,16 +52,13 @@ def tile_list_gmu_relu_gate_kernel(
         list1 = keep.tile([P, J // STRIPE], U16, name="list1")
         list2 = keep.tile([P, J // STRIPE], U16, name="list2")
         v_scale_rows = placed.tile([P, T], U8, name="v_scale_rows", offset=V_ROWS_AT, align_bytes=64)
-        v2_scale_rows = keep.tile([P, T], U8, name="v2_scale_rows", align_bytes=64)
+        v2_scale_rows = placed.tile([P, T], U8, name="v2_scale_rows", offset=V2_ROWS_AT, align_bytes=64)
         w_rows = keep.tile([BLOCKS, W_PLANES, N], U8, name="w_rows", align_bytes=64)
-        wv_w = keep.tile([P, 2, 2 * N], U8, name="wv_w", align_bytes=64)
         picked_rows = keep.tile([P, 2, J], U8, name="picked_rows", align_bytes=64)
         w_planes = keep.tile([P, W_PLANES, N], U8, name="w_planes", align_bytes=64)
         wt_plane = keep.tile([P, N], U8, name="wt_plane", align_bytes=64)
-        b_pos = keep.tile([P, N // P], F32, name="b_pos")
         b_rows = keep.tile([P, P], F32, name="b_rows")
         ident = keep.tile([P, P], F32, name="ident")
-        b_neg = keep.tile([P, N // P], F32, name="b_neg")
         picked_planes = keep.tile([P, 2, 2 * J], U8, name="picked_planes", align_bytes=64)
         picked_v = [keep.tile([P, 2, HALF], U16, name="picked_v%d" % h, align_bytes=64) for h in range(2)]
         v_words = keep.tile([P, T], U32, name="v_words", align_bytes=64)
@@ -67,26 +66,21 @@ def tile_list_gmu_relu_gate_kernel(
 
         nc.vector.memset(v2_scale_rows[:].bitcast(I32), 0)
         nc.vector.memset(v_scale_rows[0:SCALE_ROWS, :].bitcast(I32), 0)
-        nc.gpsimd.memset(w_planes[:].bitcast(I32), 0)
+        nc.vector.memset(w_planes[:].bitcast(I32), 0)
         nc.gpsimd.memset(b_rows[:], 0.0)
         nc.gpsimd.dma_start(b_rows[0 : N // P, :], b.rearrange("(c p) -> c p", p=P))
         make_identity(nc, ident[:])
         nc.gpsimd.memset(picked_planes[:, 0, :].bitcast(I32), 0)
         nc.gpsimd.memset(picked_planes[:, 1, 0:J].bitcast(I32), 0)
 
-        def by_live_row(rows):
-            return rows.rearrange("(q r) t -> r q t", r=LIVE).bitcast(I32)
-
         nc.sync.dma_start(list1[:], offs)
-        nc.sync.dma_start(v_scale_rows[SCALE_ROWS:P:2, :].bitcast(I32), by_live_row(tab_scales[0]))
-        nc.scalar.dma_start(v_scale_rows[SCALE_ROWS + 1 : P : 2, :].bitcast(I32), by_live_row(tab_scales[1]))
+        nc.sync.dma_start(v_scale_rows[SCALE_ROWS:P, :].bitcast(I32), tab_scales.rearrange("a q t -> q a t").bitcast(I32))
+        nc.sync.dma_start(list2[:], offs2)
         nc.sync.dma_start(w_rows[:, WV_PLANE:W_PLANES, :].bitcast(I32), wv_scales.rearrange("a q n -> q a n").bitcast(I32))
         nc.scalar.dma_start(w_rows[:, ZV_PLANE:ZT_PLANE, :].bitcast(I32), zv_scales.rearrange("a q n -> q a n").bitcast(I32))
         nc.scalar.dma_start(w_rows[:, ZT_PLANE, :].bitcast(I32), zt_scales[0].bitcast(I32))
-        nc.scalar.dma_start(v2_scale_rows[SCALE_ROWS:P:2, :].bitcast(I32), by_live_row(tab2_scales[0]))
+        nc.scalar.dma_start(v2_scale_rows[SCALE_ROWS:P:2, :].bitcast(I32), tab2_scales[0].bitcast(I32))
         nc.sync.dma_start(v2_words[:].bitcast(I32), tab2_words[0].rearrange("p t c -> p (t c)").bitcast(I32))
-        nc.sync.dma_start(list2[:], offs2)
-        nc.sync.dma_start(wv_w[:].bitcast(I32), wv_words.rearrange("a p m -> p a m").bitcast(I32))
         nc.sync.dma_start(v_words[:].bitcast(I32), tab_words[0].rearrange("p t c -> p (t c)").bitcast(I32))
 
         for r in range(LIVE):
@@ -98,13 +92,15 @@ def tile_list_gmu_relu_gate_kernel(
         nc.sync.dma_start(zt_w[:].bitcast(I32), zt_words[0].bitcast(I32))
         nc.sync.dma_start(zv_w[:].bitcast(I32), zv_words.rearrange("a p n c -> p a (n c)").bitcast(I32))
         nc.vector.tensor_copy(picked_rows[:, 1, :], v2_scale_rows[:].indirect(list2[:]))
-        for r in range(LIVE):
-            first = SCALE_ROWS + 2 * LIVE * r
+        for quad in (0, 2, 1, 3):
+            first = SCALE_ROWS + 2 * LIVE * quad
             nc.sync.dma_start(
-                picked_planes[r:P:QUAD, :, :].bitcast(I32),
+                picked_planes[QUAD * quad : QUAD * quad + LIVE, :, :].bitcast(I32),
                 picked_rows[first : first + 2 * LIVE, :, :].rearrange("p s j -> p (s j)").bitcast(I32),
             )
-        wt_raw = keep.tile([P, PACK, N], F32, name="wt_raw", tag="v2_scale_rows", align_bytes=64)
+        wv_w = placed.tile([P, 2, 2 * N], U8, name="wv_w", offset=WV_AT, align_bytes=64)
+        nc.sync.dma_start(wv_w[:].bitcast(I32), wv_words.rearrange("a p m -> p a m").bitcast(I32))
+        wt_raw = placed.tile([P, PACK, N], F32, name="wt_raw", offset=WT_AT, align_bytes=64)
         nc.sync.dma_start(wt_raw[:], wt.rearrange("(p j) n -> p j n", j=PACK))
 
         def entries(list_tile, start, stop):
@@ -127,6 +123,8 @@ def tile_list_gmu_relu_gate_kernel(
         )
         b_turned = psum.tile([P, HALF], F32, name="b_turned", tag="hv", bufs=H_BANKS)
         nc.tensor.transpose(b_turned[:, 0:P], b_rows[:], ident[:])
+        b_pos = placed.tile([P, N // P], F32, name="b_pos", offset=B_POS_AT, align_bytes=64)
+        b_neg = placed.tile([P, N // P], F32, name="b_neg", offset=B_NEG_AT, align_bytes=64)
         nc.vector.tensor_copy(b_pos[:], b_turned[:, 0 : N // P])
         nc.vector.tensor_scalar_mul(b_neg[:], b_turned[:, 0 : N // P], -1.0)
         v2_planes = [picked_planes[:, 0, J + HALF * h : J + HALF * (h + 1)] for h in range(2)]
@@ -201,7 +199,7 @@ def tile_list_gmu_relu_gate_kernel(
             return factor
 
         g_tiles = []
-        for i, tag in enumerate(("picked_rows", "v_words", "v2_words", "v2_scale_rows")):
+        for i, tag in enumerate(("picked_rows", "v_words", "v2_words")):
             g_tiles.append(keep.tile([P, T], F32, name="g%d" % i, tag=tag, align_bytes=64))
             nc.sync.dma_start(g_tiles[i][:], gT[P * i : P * (i + 1), :])
 
@@ -250,9 +248,11 @@ def tile_list_gmu_relu_gate_kernel(
             )
         first_product(0)
         quantise_wt()
-        first_product(1)
-        second_product(0, "gate1")
+        g_tiles.append(placed.tile([P, T], F32, name="g3", offset=WT_AT, align_bytes=64))
+        nc.sync.dma_start(g_tiles[3][:], gT[3 * P : 4 * P, :])
+        second_product(0, "part_t0")
         add_on_gpsimd(0)
+        first_product(1)
         for unit in range(1, len(units)):
             if unit in REST_UNITS:
                 rest_form(unit)

from contextlib import ExitStack

import concourse.mybir as mybir
from concourse.masks import make_identity

K, L, N, T, J = 1024, 512, 512, 2048, 1024
FLOPS = 2 * N * J * (2 * K + 2 * L)

F32 = mybir.dt.float32
BF16 = mybir.dt.bfloat16
I32 = mybir.dt.int32
U32 = mybir.dt.uint32
U16 = mybir.dt.uint16
U8 = mybir.dt.uint8
FP8X4 = mybir.dt.float8_e4m3fn_x4
FP4X4 = mybir.dt.float4_e2m1fn_x4
ACT = mybir.ActivationFunctionType
ALU = mybir.AluOpType

P = 128
PACK = 4
HALF = 512
STRIPE = 16
BLOCKS = 16
QUAD = 32
LIVE = 4
SCALE_ROWS = P - 2 * BLOCKS
ZV_PLANE, ZT_PLANE, WV_PLANE, W_PLANES = 0, 2, 3, 5
WT_G_AT, PAIRS_AT, V2_PICK1_AT = 0, 1024, 2048
ZV_AT, V_ROWS_AT, ZT_AT = 4096, 8128, 8192
B_RAW_AT, V2_PICK0_AT = 10240, 10240
WT_S_AT = 18432
WV_AT, V2_ROWS_AT, WT_AT = 20480, 22464, 24448
B_POS_AT, B_NEG_AT = 22528, 22592
Z_BANKS, H_BANKS = 2, 3
REST_UNITS, GPSIMD_ADDS, GPSIMD_FINISHES = (2,), 4, 2
GATHER_AFTER = {1: 0, 2: 1}
BACK_TAG, BACK_BUFS, RES_AFTER = "ht", 3, 7


def tile_list_gmu_relu_gate_kernel(
    tc, tab_words, tab_scales, tab2_words, tab2_scales, zv_words, zv_scales, zt_words, zt_scales,
    b, wv_words, wv_scales, wt, gT, offs, offs2, out,
):
    nc = tc.nc
    with ExitStack() as ctx:
        keep = ctx.enter_context(tc.tile_pool(name="keep", bufs=1))
        placed = ctx.enter_context(tc.tile_pool(name="placed", bufs=1))
        work = ctx.enter_context(tc.tile_pool(name="work", bufs=2))
        psum = ctx.enter_context(tc.psum_pool(name="psum", bufs=1))

        list1 = keep.tile([P, J // STRIPE], U16, name="list1")
        list2 = keep.tile([P, J // STRIPE], U16, name="list2")
        v_scale_rows = placed.tile([P, T], U8, name="v_scale_rows", offset=V_ROWS_AT, align_bytes=64)
        v2_scale_rows = placed.tile([P, T], U8, name="v2_scale_rows", offset=V2_ROWS_AT, align_bytes=64)
        w_rows = keep.tile([BLOCKS, W_PLANES, N], U8, name="w_rows", align_bytes=64)
        picked_rows = keep.tile([P, 2, J], U8, name="picked_rows", align_bytes=64)
        w_planes = keep.tile([P, W_PLANES, N], U8, name="w_planes", align_bytes=64)
        wt_plane = keep.tile([P, N], U8, name="wt_plane", align_bytes=64)
        b_rows = keep.tile([P, P], F32, name="b_rows")
        ident = keep.tile([P, P], F32, name="ident")
        picked_planes = keep.tile([P, 2, 2 * J], U8, name="picked_planes", align_bytes=64)
        picked_v = [keep.tile([P, 2, HALF], U16, name="picked_v%d" % h, align_bytes=64) for h in range(2)]
        v_words = keep.tile([P, T], U32, name="v_words", align_bytes=64)
        v2_words = keep.tile([P, T], U32, name="v2_words", align_bytes=64)

        nc.vector.memset(v2_scale_rows[:].bitcast(I32), 0)
        nc.vector.memset(v_scale_rows[0:SCALE_ROWS, :].bitcast(I32), 0)
        nc.vector.memset(w_planes[:].bitcast(I32), 0)
        nc.gpsimd.memset(b_rows[:], 0.0)
        nc.gpsimd.dma_start(b_rows[0 : N // P, :], b.rearrange("(c p) -> c p", p=P))
        make_identity(nc, ident[:])
        nc.gpsimd.memset(picked_planes[:, 0, :].bitcast(I32), 0)
        nc.gpsimd.memset(picked_planes[:, 1, 0:J].bitcast(I32), 0)

        nc.sync.dma_start(list1[:], offs)
        nc.sync.dma_start(v_scale_rows[SCALE_ROWS:P, :].bitcast(I32), tab_scales.rearrange("a q t -> q a t").bitcast(I32))
        nc.sync.dma_start(list2[:], offs2)
        nc.sync.dma_start(w_rows[:, WV_PLANE:W_PLANES, :].bitcast(I32), wv_scales.rearrange("a q n -> q a n").bitcast(I32))
        nc.scalar.dma_start(w_rows[:, ZV_PLANE:ZT_PLANE, :].bitcast(I32), zv_scales.rearrange("a q n -> q a n").bitcast(I32))
        nc.scalar.dma_start(w_rows[:, ZT_PLANE, :].bitcast(I32), zt_scales[0].bitcast(I32))
        nc.scalar.dma_start(v2_scale_rows[SCALE_ROWS:P:2, :].bitcast(I32), tab2_scales[0].bitcast(I32))
        nc.sync.dma_start(v2_words[:].bitcast(I32), tab2_words[0].rearrange("p t c -> p (t c)").bitcast(I32))
        nc.sync.dma_start(v_words[:].bitcast(I32), tab_words[0].rearrange("p t c -> p (t c)").bitcast(I32))

        for r in range(LIVE):
            nc.sync.dma_start(w_planes[r:P:QUAD, :, :].bitcast(I32), w_rows[r:BLOCKS:LIVE, :, :].bitcast(I32))

        nc.vector.tensor_copy(picked_rows[:, 0, :], v_scale_rows[:].indirect(list1[:]))
        zv_w = placed.tile([P, 2, N], U32, name="zv_w", offset=ZV_AT, align_bytes=64)
        zt_w = placed.tile([P, 2 * N], U8, name="zt_w", offset=ZT_AT, align_bytes=64)
        nc.sync.dma_start(zt_w[:].bitcast(I32), zt_words[0].bitcast(I32))
        nc.sync.dma_start(zv_w[:].bitcast(I32), zv_words.rearrange("a p n c -> p a (n c)").bitcast(I32))
        nc.vector.tensor_copy(picked_rows[:, 1, :], v2_scale_rows[:].indirect(list2[:]))
        for quad in (0, 2, 1, 3):
            first = SCALE_ROWS + 2 * LIVE * quad
            nc.sync.dma_start(
                picked_planes[QUAD * quad : QUAD * quad + LIVE, :, :].bitcast(I32),
                picked_rows[first : first + 2 * LIVE, :, :].rearrange("p s j -> p (s j)").bitcast(I32),
            )
        wv_w = placed.tile([P, 2, 2 * N], U8, name="wv_w", offset=WV_AT, align_bytes=64)
        nc.sync.dma_start(wv_w[:].bitcast(I32), wv_words.rearrange("a p m -> p a m").bitcast(I32))
        wt_raw = placed.tile([P, PACK, N], F32, name="wt_raw", offset=WT_AT, align_bytes=64)
        nc.sync.dma_start(wt_raw[:], wt.rearrange("(p j) n -> p j n", j=PACK))

        def entries(list_tile, start, stop):
            return list_tile[:, start // STRIPE : stop // STRIPE]

        def gather(picked, window, list_tile, h):
            nc.vector.tensor_copy(picked[:], window[:].indirect(entries(list_tile, h * HALF, (h + 1) * HALF)))
            return picked

        def gather_v(h):
            pairs = placed.tile([P, HALF], U32, name="pairs%d" % h, offset=PAIRS_AT, align_bytes=64)
            gather(pairs, v_words, list1, h)
            nc.vector.tensor_copy(picked_v[h][:], pairs[:].bitcast(U16).rearrange("p (t d) -> p d t", d=2))

        picked_v2 = [gather(placed.tile([P, HALF], U32, name="first_v2", offset=V2_PICK0_AT, align_bytes=64), v2_words, list2, 0)]
        gather_v(0)
        gather_v(1)
        picked_v2.append(
            gather(placed.tile([P, HALF], U32, name="second_v2", offset=V2_PICK1_AT, align_bytes=64), v2_words, list2, 1)
        )
        b_turned = psum.tile([P, HALF], F32, name="b_turned", tag="hv", bufs=H_BANKS)
        nc.tensor.transpose(b_turned[:, 0:P], b_rows[:], ident[:])
        b_pos = placed.tile([P, N // P], F32, name="b_pos", offset=B_POS_AT, align_bytes=64)
        b_neg = placed.tile([P, N // P], F32, name="b_neg", offset=B_NEG_AT, align_bytes=64)
        nc.vector.tensor_copy(b_pos[:], b_turned[:, 0 : N // P])
        nc.vector.tensor_scalar_mul(b_neg[:], b_turned[:, 0 : N // P], -1.0)
        v2_planes = [picked_planes[:, 0, J + HALF * h : J + HALF * (h + 1)] for h in range(2)]

        units = [(i, h) for h in range(2) for i in range(N // P)]
        wt_words = keep.tile([P, N], U32, name="wt_words", align_bytes=64)
        part_v = keep.tile([P, len(units), HALF], F32, name="part_v")

        def v_passes(bank, weight_of, plane, unit, start):
            i, h = units[unit]
            for a in range(2):
                nc.tensor.matmul_mx(
                    bank[:], weight_of(a, i), w_planes[:, plane + a, P * i : P * (i + 1)],
                    picked_v[h][:, a, :].bitcast(FP4X4), picked_planes[:, a, HALF * h : HALF * (h + 1)],
                    start=(start and a == 0), stop=(a == 1),
                )

        def v2_pass(bank, weight, weight_plane, unit, stop):
            h = units[unit][1]
            nc.tensor.matmul_mx(
                bank[:], weight, weight_plane, picked_v2[h][:].bitcast(FP8X4), v2_planes[h], start=True, stop=stop
            )

        def make_hv(unit):
            hv = psum.tile([P, HALF], F32, name="hv", bufs=H_BANKS)
            v_passes(hv, lambda a, i: wv_w[:, a, 2 * P * i : 2 * P * (i + 1)].bitcast(FP4X4), WV_PLANE, unit, True)
            return hv

        def make_z(unit):
            i = units[unit][0]
            z = psum.tile([P, HALF], F32, name="z", bufs=Z_BANKS)
            v2_pass(z, zt_w[:, 2 * P * i : 2 * P * (i + 1)].bitcast(FP4X4), w_planes[:, ZT_PLANE, P * i : P * (i + 1)], unit, False)
            v_passes(z, lambda a, i: zv_w[:, a, P * i : P * (i + 1)].bitcast(FP8X4), ZV_PLANE, unit, False)
            return z

        def make_ht(unit):
            i = units[unit][0]
            ht = psum.tile([P, HALF], F32, name="ht", bufs=H_BANKS)
            v2_pass(ht, wt_words[:, P * i : P * (i + 1)].bitcast(FP8X4), wt_plane[:, P * i : P * (i + 1)], unit, True)
            return ht

        def make_rest(unit, z):
            i = units[unit][0]
            rest = keep.tile([P, HALF], F32, name="rest%d" % unit, align_bytes=64)
            nc.scalar.activation(rest[:], z[:], ACT.Sigmoid, bias=b_neg[:, i : i + 1], scale=-1.0)
            return rest

        def quantise_wt():
            cuts = [slice(0, N // 2), slice(N // 2, N)]
            wt_bf = [
                placed.tile([P, N // 2, PACK], BF16, name="wt_bf0", offset=WT_G_AT, align_bytes=64),
                placed.tile([P, N // 2, PACK], BF16, name="wt_bf1", offset=WT_S_AT, align_bytes=64),
            ]
            woven = [wt_raw[:, :, cut].rearrange("p j n -> p n j") for cut in cuts]
            nc.gpsimd.tensor_scalar(wt_bf[0][:], woven[0], 1.0, 0.0, ALU.mult, ALU.add)
            nc.scalar.copy(wt_bf[1][:], woven[1])
            for cut, rounded in zip(cuts, wt_bf):
                nc.vector.quantize_mx(
                    wt_words[:, cut].bitcast(FP8X4), wt_plane[:, cut], rounded[:].rearrange("p n j -> p (n j)")
                )

        def listed_g(i, h, cut):
            return g_tiles[i][:].indirect(entries(list1, h * HALF + cut.start, h * HALF + cut.stop))

        def store(i, h, cut, values):
            nc.sync.dma_start(out[P * i : P * (i + 1), HALF * h + cut.start : HALF * h + cut.stop], values)

        def plain_factor(unit, tag):
            i, h = units[unit]
            factor = keep.tile([P, HALF], F32, name="factor%d" % unit, tag=tag, align_bytes=64)
            nc.vector.tensor_copy(factor[:], listed_g(i, h, slice(0, HALF)))
            return factor

        g_tiles = []
        for i, tag in enumerate(("picked_rows", "v_words", "v2_words")):
            g_tiles.append(keep.tile([P, T], F32, name="g%d" % i, tag=tag, align_bytes=64))
            nc.sync.dma_start(g_tiles[i][:], gT[P * i : P * (i + 1), :])

        def finish_on_gpsimd(unit, tag):
            i, h = units[unit]
            factor = plain_factor(unit, tag)
            early = work.tile([P, HALF], F32, name="early")
            nc.gpsimd.tensor_tensor(early[:], part_v[:, unit, :], factor[:], ALU.mult)
            store(i, h, slice(0, HALF), early[:])

        part_t, factors, pending = {}, {}, {}

        def first_product(unit):
            i = units[unit][0]
            z = make_z(unit)
            hv = make_hv(unit)
            gate = keep.tile([P, HALF], F32, name="gate%d" % unit, align_bytes=64)
            bias = b_pos[:, i : i + 1]
            nc.scalar.activation(gate[:], z[:], ACT.Sigmoid, bias=bias)
            pending[unit] = make_rest(unit, z)
            nc.vector.scalar_tensor_tensor(part_v[:, unit, :], hv[:], 0.0, gate[:], ALU.max, ALU.mult)

        def second_product(unit, tag):
            part_t[unit] = keep.tile([P, HALF], F32, name="part_t%d" % unit, tag=tag, align_bytes=64)
            nc.vector.scalar_tensor_tensor(part_t[unit][:], make_ht(unit)[:], 0.0, pending[unit][:], ALU.max, ALU.mult)

        def rest_form(unit):
            rest = make_rest(unit, make_z(unit))
            part_t[unit] = keep.tile([P, HALF], F32, name="part_t%d" % unit, align_bytes=64)
            nc.scalar.activation(part_t[unit][:], make_hv(unit)[:], ACT.Relu)
            floor = keep.tile([P, 16], F32, name="floor%d" % unit, align_bytes=64)
            nc.gpsimd.memset(floor[:, 0:1], 0.0)
            nc.vector.scalar_tensor_tensor(
                part_v[:, unit, :], make_ht(unit)[:], floor[:, 0:1], part_t[unit][:], ALU.max, ALU.subtract
            )
            nc.gpsimd.tensor_tensor(part_v[:, unit, :], part_v[:, unit, :], rest[:], ALU.mult)

        def add_on_gpsimd(unit):
            nc.gpsimd.tensor_tensor(part_v[:, unit, :], part_v[:, unit, :], part_t[unit][:], ALU.add)

        warm = psum.tile([P, HALF], F32, name="warm", tag="ht", bufs=H_BANKS)
        for turn_number in range(3):
            nc.tensor.matmul_mx(
                warm[:], zt_w[:, 0 : 2 * P].bitcast(FP4X4), w_planes[:, ZT_PLANE, 0:P],
                picked_v2[0][:].bitcast(FP8X4), w_planes[:, ZT_PLANE, :], start=True, stop=True,
            )
        first_product(0)
        quantise_wt()
        g_tiles.append(placed.tile([P, T], F32, name="g3", offset=WT_AT, align_bytes=64))
        nc.sync.dma_start(g_tiles[3][:], gT[3 * P : 4 * P, :])
        second_product(0, "part_t0")
        add_on_gpsimd(0)
        first_product(1)
        for unit in range(1, len(units)):
            if unit in REST_UNITS:
                rest_form(unit)
            else:
                if unit > 1:
                    first_product(unit)
                second_product(unit, "part_t%d" % unit)
            if unit < GPSIMD_ADDS:
                add_on_gpsimd(unit)
            if unit in GATHER_AFTER:
                later = GATHER_AFTER[unit]
                tag = ("floor%d" if unit in REST_UNITS else "rest%d") % unit
                if later < GPSIMD_FINISHES:
                    finish_on_gpsimd(later, tag)
                else:
                    factors[later] = plain_factor(later, tag)

        blocks = [slice(P * c, P * (c + 1)) for c in range(HALF // P)]
        totals = [part_v[:, unit, :] for unit in range(GPSIMD_ADDS)]

        def turn(unit):
            turned = psum.tile([P, HALF], F32, name="turned", tag="hv", bufs=H_BANKS)
            for block in blocks:
                for piece, first in ((part_v[:, unit, block], True), (part_t[unit][:, block], False)):
                    nc.tensor.matmul(turned[:, block], piece, ident[:], start=first, stop=not first, is_transpose=True)
            turned_sum = work.tile([P, HALF], F32, name="turned_sum", bufs=3)
            nc.scalar.copy(turned_sum[:], turned[:])
            return turned_sum

        def turn_back(unit, turned_sum):
            back = psum.tile([P, HALF], F32, name="back", tag=BACK_TAG, bufs=BACK_BUFS)
            for block in blocks:
                nc.tensor.transpose(back[:, block], turned_sum[:, block], ident[:])
            if unit in factors:
                totals.append(back[:])
            else:
                total = work.tile([P, HALF], F32, name="total", bufs=len(units) - GPSIMD_ADDS)
                nc.scalar.copy(total[:], back[:])
                totals.append(total[:])

        waiting = turn(GPSIMD_ADDS)
        for unit in range(GPSIMD_ADDS, len(units)):
            ahead = turn(unit + 1) if unit + 1 < len(units) else None
            turn_back(unit, waiting)
            waiting = ahead

        res = keep.tile([P, len(units), HALF], F32, name="res", tag="rest%d" % RES_AFTER, align_bytes=64)
        for unit in range(GPSIMD_FINISHES, len(units)):
            i, h = units[unit]
            pieces = 2 if unit == len(units) - 1 else 1
            for piece in range(pieces):
                cut = slice(piece * HALF // pieces, (piece + 1) * HALF // pieces)
                factor = factors[unit][:, cut] if unit in factors else listed_g(i, h, cut)
                nc.vector.tensor_tensor(res[:, unit, cut], factor, totals[unit][:, cut], ALU.mult)
                store(i, h, cut, res[:, unit, cut])
